import numpy as np, ml_dtypes
CORES = [2,3,42,43,82,83,122,123]
N = 8
BF = ml_dtypes.bfloat16
def gentries(a):
    return np.ascontiguousarray(a.reshape(8, 16, -1).transpose(0, 2, 1)).reshape(8, -1)
def gtable(e):
    e = np.asarray(e); return np.ascontiguousarray(e.reshape(8, -1, 16).transpose(0, 2, 1)).reshape(128, -1).astype(np.int32)
W, K, TV, S, RO, QV = 2048, 960, 3, 3, 3, 17
CH = 16
def sgn(rng, *shape):
    return 2.0 * rng.integers(0, 2, shape) - 1.0
def pay(rng, *shape):
    return sgn(rng, *shape) * (0.5 + 0.5 * rng.random(shape))
def weights(rng, *shape):
    return (0.25 + 0.75 * rng.random(shape)) * (rng.random(shape) > 0.0625)
def names(rng):
    o = np.argsort(rng.random((N, 8, TV, W)), axis=-1)[..., :2 * K]
    return o[..., :K].copy(), o[..., K:].copy()
def plain(rng):
    th = pay(rng, N, 8, 16, W); va = 0.875 * th + pay(rng, N, 8, 16, W)
    a, b = names(rng)
    return th, va, pay(rng, N, 8, 16, K), weights(rng, N, 8, 16, K), a, b
def put(x):
    x = np.where(np.abs(x) < 2.0 ** -20, 0.0, x)
    return np.ascontiguousarray(x.reshape(N, 128, -1)).astype(np.float32).astype(BF)
def near(x):
    return np.where(np.abs(x) < 2.0 ** -20, 0.0, x).astype(np.float32).astype(BF).astype(np.float64)
def pack(th, va, yt, wt, a, b):
    return {"th": put(th), "va": put(va), "yt": put(yt), "wt": put(wt), "an": np.stack([gtable(v.reshape(8, TV * K)) for v in a]),
            "bn": np.ascontiguousarray(b.reshape(N, 8 * TV, K)).astype(np.int32)}
def residues(rng, x, g):
    th, va, yt, wt, a, b = x; n = 2 * (K // TV); top = TV * (TV - 1) // 2
    fac = np.concatenate([np.arange(1, TV), np.array([-top])])
    m = rng.integers(128, 192, (16, n)); k = rng.integers(1, 63 // top + 1, (16, n)) * (2 * rng.integers(0, 2, (16, n)) - 1); s = sgn(rng, 16, n) * 2.0 ** -8
    col = np.stack([rng.permutation(W)[:2 * K].reshape(TV, n) for q in range(N)])
    wt[:, g] = 0.0
    for q in range(N):
        for i in range(TV):
            th[q, g][:, col[q, i]] = s * m; va[q, g][:, col[q, i]] = s * (m - fac[i] * k)
    for r in range(N):
        js = rng.permutation(K).reshape(TV, K // TV)
        for i in range(TV):
            sl = rng.permutation(n)
            for t in range(TV):
                v = col[(r + S * t) % N, (i + t) % TV][sl]
                a[r, g, t, js[i]] = v[:K // TV]; b[r, g, t, js[i]] = v[K // TV:]
def first(tab, va, yt, wt, a, b):
    fa = np.zeros((TV, N, 16, K)); fb = np.zeros((TV, N, 16, K)); keep = []; tab = tab.copy()
    for t in range(TV):
        own = (np.arange(N) - S * t) % N; i1 = a[own, t][:, None, :]; i2 = b[own, t][:, None, :]
        p1 = np.take_along_axis(tab, i1, 2); p2 = np.take_along_axis(tab, i2, 2)
        er = p1 * p2 - yt[own]; w8 = 0.125 * wt[own]
        np.put_along_axis(tab, i1, p1 - w8 * er * p2, 2); np.put_along_axis(tab, i2, p2 - w8 * er * p1, 2)
        fa[t][own] = 0.125 * er * p2; fb[t][own] = 0.125 * er * p1
        keep.append((own, i1, i2, w8, p1, p2, er))
    dd = tab - va; hh = np.zeros((N, 16, K))
    for t in range(TV - 1, -1, -1):
        own, i1, i2, w8, p1, p2, er = keep[t]
        d1 = np.take_along_axis(dd, i1, 2); d2 = np.take_along_axis(dd, i2, 2); mm = p1 * p2 + er
        hh[own] = hh[own] - fa[t][own] * d1 - fb[t][own] * d2
        np.put_along_axis(dd, i1, d1 - w8 * (p2 * p2 * d1 + mm * d2), 2); np.put_along_axis(dd, i2, d2 - w8 * (mm * d1 + p1 * p1 * d2), 2)
    return hh, fa, fb
def knots(rng, x, g):
    th, va, yt, wt, a, b = x; M = min(K // 3, (W - 2 * K) // (2 * (TV - 1))); n = 2 * M * (TV - 1)
    cols = np.stack([rng.permutation(W) for q in range(N)]); prv = cols[:, :n].reshape(N, TV - 1, 2, M)
    js = np.stack([rng.permutation(K) for q in range(N)])
    for q in range(N):
        th[q, g][:, prv[q, :, 0].reshape(-1)] = sgn(rng, 16, n // 2) * (0.75 + 0.25 * rng.random((16, n // 2)))
        th[q, g][:, prv[q, :, 1].reshape(-1)] = 0.0625 * pay(rng, 16, n // 2)
        va[q, g][:, cols[q, :n]] = 0.0
    for r in range(N):
        for t in range(TV):
            q = (r + S * t) % N; v = rng.permutation(cols[q, n:]); k = 0 if t == 0 else M; i = js[r, k:]
            a[r, g, t, i] = v[:K - k]; b[r, g, t, i] = v[K - k:2 * (K - k)]
            if t > 0:
                a[r, g, t, js[r, :M]] = prv[q, t - 1, 0]; b[r, g, t, js[r, :M]] = prv[q, t - 1, 1]
    for z in (th, va, yt, wt): z[:, g] = near(z[:, g])
    hh, fa, fb = first(th[:, g], va[:, g], yt[:, g], wt[:, g], a[:, g], b[:, g])
    for r in range(N):
        o = js[r, :M]; rest = hh[r][:, o]
        for f, side in ((fb, 1), (fa, 0)):
            for t in range(1, TV):
                q = (r + S * t) % N; cf = f[t, r][:, o]
                v = near(np.clip(np.divide(-rest, cf), -2.0, 2.0))
                va[q, g][:, prv[q, t - 1, side]] = v; rest = rest + cf * v
def links(rng):
    n = 2 ** 19; one = np.float32; c = one(0.125)
    w0 = near(0.75 + 0.25 * rng.random(n)).astype(one); w1 = near(0.5 + 0.5 * rng.random(n)).astype(one)
    y0 = near(1.5 + 0.5 * rng.random(n)).astype(one); p = near(1.5 + 0.5 * rng.random(n)).astype(one)
    u1 = c * (w0 * (y0 * p)); pr = u1 * p; p64 = pr.astype(np.float64)
    y1 = near(np.minimum(1.0 + p64 + np.minimum(p64, 1.0 - p64) * rng.random(n), 2.0)).astype(one)
    er = pr - y1; u2 = u1 - c * (w1 * (er * p)); p2 = p - c * (w1 * (er * u1)); m = pr + er; wrong = one(2) * er + y1
    k = 0.125 * w1.astype(np.float64); s = 1.0 - k * p.astype(np.float64) * p.astype(np.float64); km = k * np.where(m == 0, one(1), m).astype(np.float64)
    vu = near(np.clip(u2 - np.divide(km * p2, s), -2.0, 2.0)).astype(one); d1 = u2 - vu
    vv = near(np.clip(p2 - np.divide(d1 * s, km), -2.0, 2.0)).astype(one); d2 = p2 - vv
    x1 = d1 - c * (w1 * ((p * p) * d1 + m * d2)); x2 = d1 - c * (w1 * ((p * p) * d1 + wrong * d2))
    hit = np.flatnonzero((x1 > 0) & (x2 <= 0))
    if len(hit) == 0: hit = np.array([int(np.argmin(np.abs(x1)))])
    i = hit[rng.integers(0, len(hit), (N, CH, 16))]; s1 = sgn(rng, N, CH, 16); s2 = sgn(rng, N, CH, 16)
    return s1 * y0[i], w0[i], s1 * y1[i], w1[i], s2 * p[i], s1 * s2 * vu[i], s2 * vv[i]
def halves(rng, x, g):
    th, va, yt, wt, a, b = x; y0, w0, y1, w1, p, vu, vv = links(rng); n = K - 2 * CH
    cols = np.stack([rng.permutation(W) for q in range(N)]); js = np.stack([rng.permutation(K) for q in range(N)])
    for q in range(N):
        u = cols[q, :CH]; v = cols[q, CH:2 * CH]; z = cols[q, 2 * CH:6 * CH]; r = (q - S) % N; j0 = js[q, :CH]; j1 = js[r, CH:2 * CH]
        th[q, g][:, z] = 0.0; va[q, g][:, z] = 0.0
        th[q, g][:, u] = 0.0; va[q, g][:, u] = vu[q].T
        th[q, g][:, v] = p[q].T; va[q, g][:, v] = vv[q].T
        yt[q, g][:, j0] = y0[q].T; wt[q, g][:, j0] = w0[q].T
        yt[r, g][:, j1] = y1[q].T; wt[r, g][:, j1] = w1[q].T
    for r in range(N):
        for t in range(TV):
            q = (r + S * t) % N; z = rng.permutation(cols[q, 2 * CH:6 * CH]); v = rng.permutation(cols[q, 6 * CH:])
            a[r, g, t, js[r, 2 * CH:]] = v[:n]; b[r, g, t, js[r, 2 * CH:]] = v[n:2 * n]
            for i in range(2):
                j = js[r, i * CH:(i + 1) * CH]; o = z[2 * CH * i:2 * CH * (i + 1)]
                if t == i: o = cols[q, :2 * CH]
                a[r, g, t, j] = o[:CH]; b[r, g, t, j] = o[CH:]
def setup_inputs(rng):
    return pack(*plain(rng))
def sized(rng, n):
    return sgn(rng, N, 8, 16, n) * (0.8 + 0.2 * rng.random((N, 8, 16, n))) * rng.choice(np.array([0.625, 0.8, 1.0]), (N, 8, 1, n))
def setup_inputs_spread(rng):
    u = rng.random((N, 8, 1, W))
    th = sized(rng, W)
    th = np.where(u < 0.03, 2.0 ** -20 * sgn(rng, N, 8, 16, W), np.where(u > 0.98, 0.0, th))
    va = 0.875 * th + sized(rng, W)
    va = np.where((u > 0.5) & (u < 0.53), 0.0, va)
    yt = sized(rng, K)
    yt = np.where((rng.random((N, 8, 1, K)) < 0.04) | (rng.random((N, 8, 16, K)) < 0.04), 0.0, yt)
    a, b = names(rng)
    return pack(th, va, yt, weights(rng, N, 8, 16, K), a, b)
def setup_inputs_ends(rng):
    o = np.concatenate([np.arange(K), np.arange(W - K, W)])[np.argsort(rng.random((N, 8, TV, 2 * K)), axis=-1)]
    for r in range(N):
        for g in range(8):
            for t in range(TV):
                v = o[r, g, t]; i, n1, n2 = (0, 0, W - 1) if g % 2 == 0 else (K - 1, W - 1, 0)
                for place, num in ((i, n1), (K + i, n2)):
                    s = int(np.flatnonzero(v == num)[0]); old = int(v[place]); v[place] = num; v[s] = old
    for r in range(N):
        for g in range(8):
            i, n1, n2 = (0, 0, W - 1) if g % 2 == 0 else (K - 1, W - 1, 0)
            o[r, g, :, i] = n1; o[r, g, :, K + i] = n2
    a, b = o[..., :K].copy(), o[..., K:].copy()
    th = 2.0 * sgn(rng, N, 8, 16, W); same = np.array([0.7, 0.75, 0.8, 0.85, 0.7, 0.75, 0.8, 0.85]).reshape(1, 8, 1, 1)
    va = th * np.where(rng.random(th.shape) < same, 1.0, -1.0)
    yt = 2.0 * sgn(rng, N, 8, 16, K); wt = 1.0 * rng.integers(0, 2, (N, 8, 16, K))
    s7 = sgn(rng, 16, 1); s0 = sgn(rng, 16, 1)
    for x in (th, va):
        one = x[:, 7, :1].copy(); x[:, 7] = one * s7; x[:, 0] = one[..., ::-1] * s0
    for x in (yt, wt):
        one = x[:, 7, :1].copy(); x[:, 7] = one; x[:, 0] = one
    a[:, 0] = W - 1 - a[:, 7]; b[:, 0] = W - 1 - b[:, 7]
    return pack(th, va, yt, wt, a, b)
def setup_inputs_corners(rng):
    th = sgn(rng, N, 8, 16, W); yt = sgn(rng, N, 8, 16, K); wt = rng.choice(np.array([0.0, 2.0 ** -20, 0.0625]), (N, 8, 16, K))
    a, b = names(rng); kap = np.zeros((N, 8, W)); kap[:, :2] = 2.0
    for r in range(N):
        todo = [(4, rng.permutation(K)[:1 + r % 3], 2.0), (6, np.array([0, 1, K // 2, K - 2, K - 1]), 2.0)]
        if r % 2 == 1: todo.append((0, rng.integers(0, K, 1), 0.0))
        for g0, js, val in todo:
            for g in (g0, g0 + 1):
                for t in range(TV):
                    q = (r + S * t) % N
                    kap[q, g, a[r, g, t, js]] = val; kap[q, g, b[r, g, t, js]] = val
                if val > 0: yt[r, g][:, js] = -th[r, g][:, a[r, g, 0, js]] * th[r, g][:, b[r, g, 0, js]]
    return pack(th, kap[:, :, None, :] * th, yt, wt, a, b)
def setup_inputs_crowd(rng):
    th0 = pay(rng, N, 2, W); va0 = 0.875 * th0 + pay(rng, N, 2, W); y0 = pay(rng, N, 2, K); w0 = weights(rng, N, 2, K)
    nm = np.argsort(rng.random((N, TV, W)), axis=-1)[..., :2 * K]; order = np.argsort(rng.random((N, 8, W)), axis=-1)
    cls = np.stack([rng.permutation((np.arange(16) >= n).astype(np.int64)) for n in (16, 16, 15, 1, 16, 0, 1, 15)]); sg = sgn(rng, 8, 16, 1)
    th = np.zeros((N, 8, 16, W)); va = np.zeros((N, 8, 16, W)); o = np.zeros((N, 8, TV, 2 * K), np.int64)
    for q in range(N):
        for g in range(8):
            th[q, g][:, order[q, g]] = sg[g] * th0[q][cls[g]]; va[q, g][:, order[q, g]] = sg[g] * va0[q][cls[g]]
            for t in range(TV): o[q, g, t] = order[(q + S * t) % N, g][nm[q, t]]
    return pack(th, va, y0[:, cls], w0[:, cls], o[..., :K].copy(), o[..., K:].copy())
def setup_inputs_calm(rng):
    th, va, yt, wt, a, b = plain(rng)
    th[:, :4] = sgn(rng, N, 4, 16, W); u = rng.random((N, 4, 16, W))
    va[:, :4] = th[:, :4] * np.where(u < 0.25, 0.0, np.where(u < 0.55, 1.0, 2.0))
    yt[:, :4] = sgn(rng, N, 4, 16, K); wt[:, :4] = 0.0
    th[:, 2] *= 2.0 ** -20; va[:, 2] *= 2.0 ** -20; yt[:, 2] *= 2.0 ** -12
    u = rng.random((N, 16, K))
    wt[:, 6] = np.where(u < 0.25, 2.0 ** -20, np.where(u < 0.5, np.exp2(-20 + 9 * rng.random((N, 16, K))), wt[:, 6]))
    for g in (5, 7): residues(rng, (th, va, yt, wt, a, b), g)
    for g in (4, 6): knots(rng, (th, va, yt, wt, a, b), g)
    halves(rng, (th, va, yt, wt, a, b), 0)
    return pack(th, va, yt, wt, a, b)
def check_ranges(d):
    bad = []
    for k, lo, hi, least in (("th", -2.0, 2.0, 2.0 ** -20), ("va", -2.0, 2.0, 2.0 ** -20), ("yt", -2.0, 2.0, 2.0 ** -12), ("wt", 0.0, 1.0, 2.0 ** -20)):
        v = np.asarray(d[k]).astype(np.float64); s = np.abs(v)
        if not np.all((v >= lo) & (v <= hi) & ((s == 0) | (s >= least))): bad.append("range of " + k)
    for k in ("an", "bn"):
        if np.min(d[k]) < 0 or np.max(d[k]) > W - 1: bad.append("range of " + k)
    a = np.stack([gentries(v) for v in np.asarray(d["an"])]).reshape(N, 8, TV, K); b = np.asarray(d["bn"]).reshape(N, 8, TV, K)
    o = np.sort(np.concatenate([a, b], axis=-1), axis=-1)
    if np.any(o[..., 1:] == o[..., :-1]): bad.append("names of a visit (an and bn) repeat")
    if not bad and rounds(d["th"], d["va"], d["yt"], d["wt"], d["an"], d["bn"], True)[2]: bad.append("a product under 2 ** -126")
    return bad
def tiny(A, B, e, w, da, db):
    m = A * B + e; one = np.float32(1)
    pairs = ((A, B), (B, B), (A, A), (e, B), (e, A), (w, e * B), (w, e * A), (e * B, da), (e * A, db), (B * B, da), (m, db), (m, da), (A * A, db),
             (one, (e * B) * da + (e * A) * db), (w, (B * B) * da + m * db), (w, m * da + (A * A) * db))
    return any(bool(np.any((u != 0) & (v != 0) & (np.abs(u * v) < 2.0 ** -123))) for u, v in pairs)
def rounds(th, va, yt, wt, an, bn, watch):
    a = np.stack([gentries(v) for v in an]).astype(np.int64).reshape(N, 8, TV, K); b = bn.astype(np.int64).reshape(N, 8, TV, K); low = False
    for rnd in range(RO):
        ft = np.float32 if rnd < RO - 1 else np.float64
        c = ft(0.125); tab = th.astype(ft).reshape(N, 8, 16, W)
        y = yt.astype(ft).reshape(N, 8, 16, K); w = wt.astype(ft).reshape(N, 8, 16, K); kept = []
        for t in range(TV):
            own = (np.arange(N) - S * t) % N
            ia = a[own, :, t][:, :, None, :]; ib = b[own, :, t][:, :, None, :]; ww = w[own]
            A = np.take_along_axis(tab, ia, 3); B = np.take_along_axis(tab, ib, 3)
            e = A * B - y[own]
            np.put_along_axis(tab, ia, A - c * (ww * (e * B)), 3)
            np.put_along_axis(tab, ib, B - c * (ww * (e * A)), 3)
            kept.append((own, ia, ib, ww, A, B, e))
        d = tab - va.astype(ft).reshape(N, 8, 16, W); h = np.zeros((N, 8, 16, K), ft)
        for t in range(TV - 1, -1, -1):
            own, ia, ib, ww, A, B, e = kept[t]
            da = np.take_along_axis(d, ia, 3); db = np.take_along_axis(d, ib, 3)
            if watch and rnd < RO - 1: low = low or tiny(A, B, e, ww, da, db)
            h[own] = h[own] - c * ((e * B) * da + (e * A) * db)
            m = A * B + e
            np.put_along_axis(d, ia, da - c * (ww * ((B * B) * da + m * db)), 3)
            np.put_along_axis(d, ib, db - c * (ww * (m * da + (A * A) * db)), 3)
        if rnd < RO - 1:
            up = np.sum((h > 0).astype(np.int64), axis=2)
            refused = up + np.roll(up, -1, axis=1) >= QV
            for r in range(N):
                for g in range(8):
                    p = np.flatnonzero(refused[r, g])
                    if len(p) > 1: b[r, g][:, p] = b[r, g][:, np.roll(p, 1)]
    return d, h, low
def reference(th, va, yt, wt, an, bn):
    d, h, low = rounds(th, va, yt, wt, an, bn, False)
    return {"yd": d.reshape(N, 128, W).astype(np.float32), "yh": h.reshape(N, 128, K).astype(np.float32)}

def check_inputs(d):
    bad = list(check_ranges(d))
    if not bad:
        for name, y in reference(**d).items():
            for q in range(N):
                v = np.abs(np.asarray(y[q], np.float64)); s = np.sqrt(np.mean(v * v))
                if v.max() > 12 * s or s < 2.0 ** -4: bad.append('%s of rank %d is uneven or too small' % (name, q))
    return bad

@@ -1,0 +1,771 @@
+import numpy as np
+from concourse.bass import DstId, RemoteDMATransfer
+from concourse.mybir import AluOpType, ActivationFunctionType
+
+N, W, K, TV, STEP, RO = 8, 2048, 960, 3, 3, 3
+H = K // 2
+KW = K // 16
+O0, O1, O2 = W, W + 2 * K, W + 4 * K
+FAR = 10240
+JM = 8192.0
+PO = 32
+OPT = dict(m_dma=True, pe_e=True, pe_init="ab", pe_m=True, pe3=True, fuse=True, put="sssvss", get="svvssvsvsssss", pe_cp="",
+           full=True, head=160, relay=False)
+TRIES = 14000
+F32, BF, I32, U16 = "float32", "bfloat16", "int32", "uint16"
+
+SCRATCH = {}
+for _n, _c, _d in [
+        ("tw", O2, F32), ("dw", O2 + W, F32), ("wf", W, F32), ("vj", K, F32), ("thb", W, BF), ("vab", W, BF),
+        ("raw", 2 * K, BF), ("yw0", 2 * K, BF), ("yw1", 2 * K, BF), ("yw2", 2 * K, BF),
+        ("a0", K, BF), ("b0s", K, BF), ("b0", K, BF), ("a1", K, F32), ("b1", K, F32), ("a2", K, F32), ("b2", K, F32),
+        ("ab0", K, F32), ("ab1", K, F32), ("ab2", K, F32), ("ea0", K, F32), ("ea1", K, F32), ("ea2", K, F32),
+        ("eb0", K, F32), ("eb1", K, F32), ("eb2", K, F32), ("aa0", K, F32), ("bb0", K, F32), ("aa1", K, F32),
+        ("bb1", K, F32), ("bt", K, F32), ("q1", K, F32), ("xs", K, F32), ("pa", K, F32),
+        ("pb", K, F32), ("u1", K, F32), ("da", K + 8, F32), ("db", K, F32),
+        ("lu0", K, F32), ("ls0", K, F32), ("lu1", K, F32), ("ls1", K, F32),
+        ("vaa", K, BF), ("vbs", K, BF), ("vbb", K, BF), ("kr", K, F32), ("br", K, I32), ("up", K, BF),
+        ("ani", 3 * KW, I32), ("bri", KW, I32), ("n0", 2 * KW, U16), ("nb0", KW, U16), ("s1", 2 * KW, U16),
+        ("s2", 2 * KW, U16), ("r1", 2 * KW, U16), ("r2", 2 * KW, U16),
+        ("ia", 128, I32), ("fa", 128, F32), ("fb", 128, F32),
+        ("pi", 8, I32), ("pj", 8, I32), ("pf", 8, F32), ("cw", 128, F32), ("jw", 128, F32), ("j6", 6 * KW, F32),
+        ("rho", KW, U16), ("pos", KW, U16), ("rh2", 128, U16), ("po2", 128, U16), ("sw2", 128, F32),
+        ("dl", 128, U16), ("hl", 128, U16), ("gw", 2 * KW, F32),
+        ("f1", 2 * KW, U16), ("f2", 2 * KW, U16), ("g1", 2 * KW, U16), ("g0", 2 * KW, U16), ("home", 3 * KW, U16),
+        ("kw", 6 * KW, F32), ("wp", 384, F32), ("wc", 6 * KW, F32), ("iw", KW, F32),
+        ("lw1", 6 * KW, U16), ("lw2", 6 * KW, U16), ("v11", 2 * KW, U16), ("v12", 2 * KW, U16),
+        ("v21", 2 * KW, U16), ("v22", 2 * KW, U16), ("x01", KW, U16), ("x02", KW, U16), ("x11", KW, U16),
+        ("x12", KW, U16), ("x21", KW, U16), ("x22", KW, U16),
+        ("one", H, BF), ("onf", 128, F32), ("idf", 128, F32), ("idb", 128, BF), ("nif", 128, F32), ("nib", 128, BF),
+        ("vm", 128, BF), ("bm", 128, BF)]:
+    SCRATCH[_n] = ("sbuf", [128, _c], _d)
+for _i in range(4):
+    SCRATCH["ps%d" % _i] = ("psum", [128, 1024], F32)
+SIZE = {F32: 4, BF: 2, I32: 4, U16: 2}
+
+NOM = dict(cyc=0.00102, gat=1.5, sca=3.5, fix=0.06, hop=0.12, pe=0.0005, dma=2.1, gdma=1.0, rem=1.2, net=2.5, bw=70e3)
+SPREAD = [NOM, dict(NOM, gat=1.1, sca=2.0), dict(NOM, gat=2.0, sca=5.5), dict(NOM, dma=3.0, net=4.0, bw=45e3, pe=0.0007)]
+
+
+def S(name, lo=0, hi=None):
+    return (name, lo, SCRATCH[name][1][1] if hi is None else hi)
+
+
+def I(win, off):
+    return ("#", win, off)
+
+
+def ap(T, x):
+    if x[0] == "#":
+        return ap(T, x[1]).indirect(ap(T, x[2]))
+    if len(x) == 4:
+        return T[x[0]][:, x[1]:x[2]:x[3]]
+    return T[x[0]][:, x[1]:x[2]]
+
+
+def width(x):
+    if x[0] == "#":
+        return 16 * (x[2][2] - x[2][1])
+    return (x[2] - x[1] + x[3] - 1) // x[3] if len(x) == 4 else x[2] - x[1]
+
+
+def psum(x):
+    return x[0] != "#" and x[0].startswith("ps")
+
+
+def transfer(topo, dst, mask, sem, srcs, land):
+    rid, pid, _ = topo.addr(dst)
+    return RemoteDMATransfer(dst_ids=[DstId(rid=rid, pnc=pid)], dma_engine_mask=mask, remote_sem=sem, srcs=srcs, dsts=[land],
+                             alu_op=1 if len(srcs) > 1 else 0)
+
+
+def helper(T, topo, core):
+    mine = [c for c in T.cores if topo.chip(c) == topo.chip(core)]
+    free = [c for c in topo.cores_of(core) if topo.die(c) != topo.die(core) and c not in T.cores
+            and all(topo.may_write(c, d) for d in T.cores)]
+    return free[mine.index(core)]
+
+
+def build(opt):
+    ops, relays = [], []
+    sems = ["cv", "cs", "ct", "cg", "hand"]
+    wr, rd, main = {}, {}, [False]
+
+    def span(x):
+        sz = SIZE[SCRATCH[x[0]][2]]
+        b = 2048 if psum(x) else 16
+        return x[0], x[1] * sz // b * b, -(-x[2] * sz // b) * b
+
+    def add(q, fn, reads, writes, cost, kind="c", lat=None, group=None, after=(), cnt=16):
+        i = len(ops); deps = set(after)
+        rs, ws = [], []
+        for x in reads:
+            rs += [x[1], x[2]] if x[0] == "#" else [x]
+        for x in writes:
+            if x[0] == "#":
+                ws.append(x[1]); rs.append(x[2])
+            else:
+                ws.append(x)
+        for x in rs:
+            n, lo, hi = span(x)
+            deps.update(j for a, b, j in wr.get(n, []) if a < hi and lo < b)
+            if psum(x):
+                deps.update(j for a, b, j in rd.get(n, []) if a < hi and lo < b and ops[j]["q"] != q)
+        for x in ws:
+            n, lo, hi = span(x)
+            if kind != "r":
+                deps.update(j for a, b, j in wr.get(n, []) + rd.get(n, []) if a < hi and lo < b)
+        for x in rs:
+            n, lo, hi = span(x)
+            rd.setdefault(n, []).append((lo, hi, i))
+        for x in ws:
+            n, lo, hi = span(x)
+            wr[n] = [e for e in wr.get(n, []) if not (lo <= e[0] and e[1] <= hi)] + [(lo, hi, i)]
+            rd[n] = [e for e in rd.get(n, []) if e[2] == i or not (lo <= e[0] and e[1] <= hi)]
+        deps.discard(i)
+        if group is not None:
+            for j in [j for j in deps if ops[j]["group"] == group]:
+                deps.discard(j); deps.update(ops[j]["deps"])
+        if kind != "c" and group is None:
+            group = "d%d" % i
+        if group is not None and group not in sems:
+            sems.append(group)
+        ops.append(dict(q=q, fn=fn, deps=deps, cost=cost, kind=kind, lat=lat, group=group, cnt=cnt, main=main[0] and q == "v",
+                        nm=[x[:3] if x[0] != "#" else x[1] for x in writes][:1]))
+        return i
+
+    def ecost(out, ins, two):
+        n = width(out)
+        if out[0] == "#":
+            return lambda m: m["fix"] + n * m["sca"] * m["cyc"]
+        if ins and ins[0][0] == "#":
+            return lambda m: m["fix"] + n * m["gat"] * m["cyc"]
+        return lambda m: m["fix"] + max(64, n * two) * m["cyc"]
+
+    def tt(out, x, y, op):
+        two = 1 if psum(x) or psum(y) else 2
+        return add("v", lambda g, T, c: g.vector.tensor_tensor(ap(T, out), ap(T, x), ap(T, y), op), [x, y], [out], ecost(out, [x], two))
+
+    def ts(out, x, s1, op0, s2=None, op1=None):
+        col = [s for s in (s1, s2) if isinstance(s, tuple)]
+
+        def fn(g, T, c):
+            a = ap(T, s1) if isinstance(s1, tuple) else s1
+            if op1 is None:
+                return g.vector.tensor_scalar(ap(T, out), ap(T, x), a, None, op0)
+            return g.vector.tensor_scalar(ap(T, out), ap(T, x), a, ap(T, s2) if isinstance(s2, tuple) else s2, op0, op1)
+        return add("v", fn, [x] + col, [out], ecost(out, [x], 1))
+
+    def cp(out, x):
+        return add("v", lambda g, T, c: g.vector.tensor_copy(ap(T, out), ap(T, x)), [x], [out], ecost(out, [x], 1))
+
+    def fill(out, v):
+        return add("v", lambda g, T, c: g.vector.memset(ap(T, out), v), [], [out], ecost(out, [], 1))
+
+    def scan(out, d0, d1, init):
+        col = [init] if isinstance(init, tuple) else []
+        return add("v", lambda g, T, c: g.vector.tensor_tensor_scan(ap(T, out), ap(T, d0), ap(T, d1), ap(T, init) if col else init,
+                                                                    AluOpType.max, AluOpType.min), [d0, d1] + col, [out], ecost(out, [d0], 1))
+
+    def act(out, x, func=ActivationFunctionType.Copy, scale=None, bias=None):
+        def fn(g, T, c):
+            if bias is not None:
+                return g.scalar.activation(ap(T, out), ap(T, x), func, bias=bias, scale=scale)
+            if scale is None:
+                return g.scalar.activation(ap(T, out), ap(T, x), func)
+            return g.scalar.activation(ap(T, out), ap(T, x), func, scale=scale)
+        return add("s", fn, [x], [out], ecost(out, [x], 1))
+
+    def mms(parts):
+        n = sum(max(64, width(p[2])) * (4 if SCRATCH[p[2][0]][2] == F32 else 1) for p in parts)
+
+        def fn(g, T, c):
+            for out, lhs, rhs, start, stop in parts:
+                ins = g.tensor.matmul(ap(T, out), ap(T, lhs), ap(T, rhs), start, stop)
+            return ins
+        return add("t", fn, [x for p in parts for x in p[1:3]], [p[0] for p in parts], lambda m: 0.03 * len(parts) + n * m["pe"])
+
+    def mm(out, lhs, rhs, *more):
+        if more:
+            return mms([(out, lhs, rhs, True, False), (out, more[0], more[1], False, True)])
+        return mms([(out, lhs, rhs, True, True)])
+
+    def iota(out, pat, base, cm):
+        fl = SCRATCH[out[0]][2] != I32
+
+        def fn(g, T, c):
+            if fl:
+                return g.iota(ap(T, out), pat, base, cm, allow_small_or_imprecise_dtypes=True)
+            return g.iota(ap(T, out), pat, base, cm)
+        return add("g", fn, [], [out], lambda m: 0.13 + 2 * width(out) * m["cyc"])
+
+    def keep(out, x, pat, op, base, cm):
+        return add("g", lambda g, T, c: g.affine_select(ap(T, out), ap(T, x), pat, op, 0.0, base, cm), [x], [out], lambda m: 0.43)
+
+    def dma(fo, fi, reads, writes, nb, group=None, q="y"):
+        def fn(g, T, c):
+            return (g.sync if q == "y" else g.scalar).dma_start(fo(T), fi(T))
+        return add(q, fn, reads, writes, lambda m: 0.1, "d", lambda m: m["dma"] + nb / 500e3, group)
+
+    def gdma(out, src, acc=True):
+        def fn(g, T, c):
+            if acc:
+                return g.dma_start(ap(T, out), ap(T, src), accum_op=AluOpType.add)
+            return g.dma_start(ap(T, out), ap(T, src))
+        return add("g", fn, [src, out] if acc else [src], [out], lambda m: m["gdma"], "d", lambda m: m["dma"] + width(out) * 512 / 300e3)
+
+    def wrap(out, src, row, group=None):
+        return dma(lambda T: ap(T, out), lambda T: T[src[0]][row::16, src[1]:src[2]], [src], [out], 200e3, group)
+
+    def unwrap(out, row, src, group=None):
+        return dma(lambda T: T[out[0]][row::16, out[1]:out[2]], lambda T: ap(T, src), [src], [out], 200e3, group)
+
+    def send(parts, also=(), relay=False):
+        i = len(ops); hand = None
+        if relay and opt["relay"]:
+            (srcs, step, land), = parts
+            h = (land[2] - land[1]) // 2
+            parts = [([S(x[0], x[1], x[1] + h) for x in srcs], step, S(land[0], land[1], land[1] + h))]
+            upper = S(land[0], land[1] + h, land[2])
+            hold = upper if land[0].startswith("yw") else S("dw", len(relays) * h, (len(relays) + 1) * h)
+            hand = [S(x[0], x[1] + h, x[2]) for x in srcs]
+            relays.append((i, step, hold, upper)); sems.append("h%d" % i)
+        per = 8 // (1 << (len(parts) - 1).bit_length())
+        names = {}
+        for srcs, step, land in parts:
+            names.setdefault(step, []).append(land)
+
+        def fn(g, T, c):
+            tr = []; used = 0
+            for k, (srcs, step, land) in enumerate(parts):
+                dst = T.cores[(c["rank"] + step) % N]
+                mask = sum(1 << e for e in c["topo"].engines(c["core"], dst)[k * per:(k + 1) * per]); used += mask
+                tr.append(transfer(c["topo"], dst, mask, T.sem["a%d_%d" % (i, step % N)], [ap(T, s) for s in srcs], ap(T, land)))
+            if hand:
+                by = helper(T, c["topo"], c["core"])
+                eng = [e for e in c["topo"].engines(c["core"], by) if not used >> e & 1][:per]
+                tr.append(transfer(c["topo"], by, sum(1 << e for e in eng), T.sem["h%d" % i], [ap(T, s) for s in hand], ap(T, hold)))
+            return g.remote_dma_fused(tr, local_sem=T.sem["d%d" % i])
+        nb = sum(128 * width(p[0][0]) * SIZE[SCRATCH[p[0][0][0]][2]] for p in parts)
+        add("g", fn, [s for p in parts for s in p[0]] + (hand or []), list(also), lambda m: m["rem"], "x",
+            lambda m: 1.0 + nb / m["bw"], cnt=per * len(parts) * (2 if hand else 1))
+        for step, lands in names.items():
+            add("-", None, [], lands + ([upper] if hand else []), lambda m: 0.0, "r",
+                lambda m: m["net"] - 1.0 + (2.0 + m["rem"] + nb / 200e3 if hand else 0.0), "a%d_%d" % (i, step % N),
+                after=[i], cnt=per * len(lands) * (2 if hand else 1))
+
+    mul, plus, minus, mx = AluOpType.mult, AluOpType.add, AluOpType.subtract, AluOpType.max
+    Silu, Square, Ident = ActivationFunctionType.Silu, ActivationFunctionType.Square, ActivationFunctionType.Identity
+
+    def tolist(out, src, sub=0):
+        ts(out, src, 0.25 - sub, plus)
+
+    def places(out, n):
+        ts(S("ia", 0, n), S("cw", 0, n), -(n - 1) / 2.0, plus, 1.0 / n, mul)
+        ts(S("fa", 0, n), S("ia", 0, n), -(16 * n - 1) / 16.0, mul)
+        tt(S("fa", 0, n), S("fa", 0, n), S("cw", 0, n), plus)
+        ts(out, S("fa", 0, n), 16.0, mul)
+
+    fill(S("br"), 0)
+    dma(lambda T: T.ani[:], lambda T: T.an[:], [], [S("ani")], 90e3, "names")
+    dma(lambda T: T.bri[:], lambda T: T.bn[0::TV, :], [], [S("bri")], 200e3, "names")
+    for t in range(TV):
+        dma(lambda T, t=t: T.br[4 * t::16, :], lambda T, t=t: T.bn[t::TV, :], [], [S("br")], 100e3, "rows")
+    dma(lambda T: T.thb[:], lambda T: T.th[:], [], [S("thb")], 520e3, q="s")
+    dma(lambda T: T.raw[:, :K], lambda T: T.yt[:], [], [S("raw", 0, K)], 500e3, q="s")
+    dma(lambda T: T.raw[:, K:], lambda T: T.wt[:], [], [S("raw", K)], 500e3, q="s")
+    dma(lambda T: T.vab[:], lambda T: T.va[:], [], [S("vab")], 900e3)
+    iota(S("pi", 0, 1), [[0, 1]], 0, 1)
+    iota(S("cw"), [[16, 128]], 0, 0)
+    iota(S("jw"), [[1, 128]], 0, 0)
+    iota(S("wf", 0, 512), [[1, 512]], 0, 0)
+    iota(S("dw", O0, O0 + K), [[1, 16], [16, KW]], O0, 0)
+    iota(S("vj"), [[1, K]], O0 + K, 0)
+    ts(S("pj", 0, 1), S("pi", 0, 1), 15, AluOpType.bitwise_and)
+    cp(S("pf", 0, 1), S("pj", 0, 1))
+    ts(S("cw"), S("cw"), S("pf", 0, 1), plus)
+    ts(S("pf", 4, 5), S("pf", 0, 1), float(KW), mul)
+    ts(S("rho"), S("jw", 0, KW), S("pf", 4, 5), plus)
+    places(S("pos"), KW)
+    act(S("wf", 512, 1024), S("wf", 0, 512), Ident, 1.0, 512.0)
+    act(S("wf", 1024), S("wf", 0, 1024), Ident, 1.0, 1024.0)
+    cp(S("n0", 0, KW), S("ani", 0, KW))
+    cp(S("n0", KW), S("bri"))
+    cp(S("s1", 0, KW), S("ani", KW, 2 * KW))
+    cp(S("s2", 0, KW), S("ani", 2 * KW))
+    cp(S("lu1"), I(S("br"), S("pos")))
+    for t in range(TV):
+        wrap(S("wp", t * KW, (t + 1) * KW), S("lu1"), 4 * t, "wrapb")
+    cp(S("s1", KW), S("wp", KW, 2 * KW))
+    cp(S("s2", KW), S("wp", 2 * KW, 3 * KW))
+    cp(S("nb0"), S("wp", 0, KW))
+    send([([S("s1")], STEP, S("r1")), ([S("s2")], 2 * STEP, S("r2"))])
+    who = {k: list(opt[k]) for k in ("put", "get")}
+
+    def put(lst, val):
+        if who["put"].pop(0) == "v":
+            cp(I(S("wf"), lst), val)
+        else:
+            act(I(S("wf"), lst), val, Silu)
+
+    def get(out, src, f=1.0):
+        if who["get"].pop(0) == "v":
+            ts(out, src, f, mul)
+        else:
+            act(out, src, scale=f)
+
+    put(S("n0", 0, KW), S("dw", O0, O0 + K))
+    put(S("n0", KW), S("vj"))
+    sw0, sw1, l2, l1, lh = S("wc", 0, 128), S("wc", 128, 256), S("wp", 0, 128), S("wp", 128, 256), S("wp", 256, 384)
+    wrap(sw0, S("wf"), 0)
+    get(S("yw0", 0, K), I(S("raw", 0, K), S("rho")))
+    get(S("b0"), I(S("thb"), S("n0", 0, KW)))
+    get(S("a0"), I(S("b0"), S("rho")))
+    get(S("yw0", K), I(S("raw", K), S("rho")), 0.125)
+    get(S("b0s"), I(S("thb"), S("n0", KW)))
+    send([([S("yw0")], STEP, S("yw1"))], relay=True)
+    send([([S("yw0")], 2 * STEP, S("yw2"))], relay=True)
+    gdma(S("tw", 0, W), S("thb"), False)
+    fill(S("onf"), 1.0)
+    keep(S("idf"), S("onf"), [[-1, 128]], AluOpType.is_equal, 0, 1)
+    cp(S("idb"), S("idf"))
+    if opt["pe_e"] or opt["pe_m"]:
+        ts(S("nib"), S("idf"), -1.0, mul)
+    if opt["pe_init"] or opt["pe3"]:
+        ts(S("nif"), S("idf"), -1.0, mul)
+    for lo in range(O1, O2 + 2 * K, K):
+        iota(S("dw", lo, lo + K), [[1, 16], [16, KW]], lo if lo < O2 else lo - O2 + FAR, 0)
+    ta = [S("n0", 0, KW), S("r1", 0, KW), S("r2", 0, KW)]
+    tb = [S("nb0"), S("r1", KW), S("r2", KW)]
+
+    def lookup(out, t, row):
+        get(S("lu1"), I(S("wf"), ta[t]))
+        wrap(S("gw", 0, KW), S("lu1"), row)
+        tolist(S(out, 0, KW), S("gw", 0, KW))
+        get(S("ls1"), I(S("wf"), tb[t]))
+        wrap(S("gw", KW), S("ls1"), row)
+        tolist(S(out, KW), S("gw", KW))
+
+    lookup("f1", 1, 0)
+    put(ta[1], S("dw", O1, O1 + K))
+    put(tb[1], S("dw", O1 + K, O2))
+    wrap(sw1, S("wf"), 0)
+    lookup("f2", 2, 0)
+    tolist(S("dl"), sw1)
+    put(ta[2], S("dw", O2, O2 + K))
+    put(tb[2], S("dw", O2 + K, O2 + 2 * K))
+    wrap(S("sw2"), S("wf"), 0)
+    act(S("raw"), I(S("vab"), S("r2")))
+    act(S("vaa"), I(S("raw", 0, K), S("rho")))
+    act(S("vbs"), I(S("raw", K), S("rho")))
+    ts(S("pf", 6, 7), S("pf", 0, 1), 128.0, mul)
+    ts(S("rh2"), S("jw"), S("pf", 6, 7), plus)
+
+    def overlay(out, below, sw, base, to):
+        ts(S("fa"), sw, 0.5 - base, plus, 65536.0, mul)
+        if to != base:
+            ts(sw, sw, float(to - base), plus)
+        tt(S("fa"), S("fa"), sw, AluOpType.min)
+        tt(out, below, S("fa"), mx)
+
+    ts(S("sw2"), S("sw2"), float(O0 - FAR), plus)
+    tt(l2, S("cw"), S("sw2"), mx)
+    overlay(l1, l2, sw1, O1, O1)
+    overlay(lh, l1, sw0, O0, O2)
+    for row, src in ((0, l2), (4, l1), (8, lh)):
+        unwrap(S("wf"), row, src, "unl")
+    lookup("g1", 1, 0)
+    lookup("g0", 0, 4)
+    places(S("po2"), 128)
+    act(S("dw", O2), I(S("wf"), S("po2")))
+    wrap(S("sw2"), S("dw", O2), 8)
+    tolist(S("hl"), S("sw2"))
+    send([([S("f1", KW)], -STEP, S("home", 0, KW)), ([S("g1", KW)], -STEP, S("home", KW, 2 * KW)),
+          ([S("f2", KW)], -2 * STEP, S("home", 2 * KW))])
+    rows = [4, 8, 12, 2, 6, 0]
+    iota(S("j6"), [[0, 6], [int(JM), KW]], 0, 0)
+    ts(S("pf", 2, 3), S("pf", 0, 1), KW * JM, mul)
+    ts(S("j6"), S("j6"), S("pf", 2, 3), plus)
+    cp(S("kw", 0, KW), S("rho"))
+    cp(S("kw", KW, 2 * KW), S("g0", KW))
+    cp(S("kw", 2 * KW, 5 * KW), S("home"))
+    cp(S("kw", 5 * KW), S("cw", 0, KW))
+    tt(S("kw"), S("kw"), S("j6"), plus)
+    iota(S("kr"), [[0, K]], 0, 0)
+    for i in range(6):
+        unwrap(S("kr"), rows[i], S("kw", i * KW, (i + 1) * KW), "unk0")
+    iota(S("one"), [[0, H]], 1, 0)
+    fill(S("bm"), -33.0 * 2 ** 17)
+    fill(S("vm"), 2.0 ** 25)
+    keep(S("vm"), S("vm"), [[-16, 8], [0, 16]], AluOpType.is_ge, 0, 1)
+    keep(S("vm"), S("vm"), [[16, 8], [0, 16]], AluOpType.is_gt, 32, -1)
+    add("v", lambda g, T, c: g.vector.memset(T.vm[0:16, 112:128], 2.0 ** 25), [], [S("vm", 112)], lambda m: 0.13)
+    if opt["pe_m"]:
+        ts(S("jw"), S("idf"), 2.0, mul)
+
+    def c_(name, c, base=0):
+        return S(name, base + c[0], base + c[1])
+
+    def o_(x, c):
+        return S(x[0], x[1] + c[0] // 16, x[1] + c[1] // 16)
+
+    def coef(sq, x, P, yw):
+        act(S(P, PO, PO + K), S(x), Square)
+        tt(S(sq), S(yw, K), S(P, PO, PO + K), mul)
+        act(S(sq), S(sq), Ident, -1.0, 1.0)
+
+    main[0] = True
+    two = [(0, H), (H, K)]
+    wide = [(0, K)] if opt["full"] else two
+    three = [(0, opt["head"]), (opt["head"], H), (H, K)]
+
+    for k in range(RO):
+        last = k == RO - 1
+        R = ["ps%d" % ((i + k) % 4) for i in range(4)]
+        if k == 0:
+            fb = [None, S("f1", KW), S("f2", KW)]; gb = [S("g0", KW), S("g1", KW)]
+        else:
+            fb = [None, S("v1%d" % k, 0, KW), S("v2%d" % k, 0, KW)]; gb = [S("lw%d" % k, KW, 2 * KW), S("v1%d" % k, KW)]
+        fa = [None, S("f1", 0, KW), S("f2", 0, KW)]; ga = [S("g0", 0, KW), S("g1", 0, KW)]
+        bn = ["b0s" if k == 0 else "b0", "b1", "b2"]
+        vb = "vbs" if k == 0 else "vbb"
+        lu, ls = "lu%d" % (k % 2), "ls%d" % (k % 2)
+
+        def back(win, base, t):
+            if k > 0:
+                act(S(win, base, base + K), I(S("bt"), S("x%d%d" % (t, k))))
+
+        for t in range(TV):
+            E, C, X = R[1 if t != 1 else 0], R[2], R[3]
+            a, b, yw, ab, ea, eb = "a%d" % t, bn[t], "yw%d" % t, "ab%d" % t, "ea%d" % t, "eb%d" % t
+            pe3 = last and t == 2 and opt["pe3"]
+            for c in two:
+                if not opt["pe_e"]:
+                    mm(c_(E, c, PO), S("idb"), c_(yw, c))
+                mm(c_(C, c, PO), S("idb"), c_(yw, c, K))
+            if t == 0:
+                win, lst = (S("thb"), S("n0", KW)) if k == 0 else (S("b0s"), S("lw%d" % k, 5 * KW))
+            else:
+                win, lst = S("tw", 0, O1 if t == 1 else O2), fb[t]
+                for c in three:
+                    act(c_(a, c), I(win, o_(fa[t], c)))
+            if t > 0 or k > 0:
+                for c in two:
+                    act(c_(b, c), I(win, o_(lst, c)))
+            if t == 2:
+                if k == 0:
+                    act(S("thb"), I(S("vab"), S("rh2")))
+                act(S("dw", 0, W), I(S("tw"), S("dl")), scale=-1.0)
+                gdma(S("dw", 0, W), S("thb"))
+                if k > 0:
+                    act(S("vbb"), I(S("vbs"), S("v2%d" % k, KW)))
+            base = O0 + 2 * K * t
+            for c in (three if t > 0 else two):
+                tt(c_(ab, c), I(win, o_(lst, c)), c_(a, c), mul)
+            for c in two:
+                if opt["pe_e"]:
+                    mm(c_(E, c, PO), S("idf"), c_(ab, c), S("nib"), c_(yw, c))
+                else:
+                    tt(c_(E, c, PO), c_(ab, c), c_(E, c, PO), minus)
+            for c in two:
+                tt(c_(ea, c), c_(E, c, PO), c_(a, c), mul)
+            if pe3:
+                for P, v, x in ((R[3], vb, b), (R[0], "vaa", a)):
+                    for c in two:
+                        mms([(c_(P, c, PO), S("idb"), c_(v, c), True, False), (c_(P, c, PO), S("nif"), c_(x, c), False, False)])
+            for c in two:
+                tt(c_("bt", c) if pe3 else c_(X, c, PO), c_(ea, c), c_(C, c, PO), mul)
+            for c in two if not pe3 else ():
+                if t == 2:
+                    out = c_("bt", c) if "b" in opt["pe_init"] else c_(X, c, PO)
+                else:
+                    out = c_("tw", c, base + K) if k == 0 else c_("bt", c)
+                tt(out, c_(b, c), c_(X, c, PO), minus)
+            if t < 2:
+                back("tw", base + K, t)
+            for c in two:
+                tt(c_(eb, c), c_(E, c, PO), c_(b, c), mul)
+            for c in two:
+                tt(c_("q1", c) if pe3 else c_(C, c, PO), c_(eb, c), c_(C, c, PO), mul)
+            for c in two if not pe3 else ():
+                out = c_("tw", c, base) if t < 2 else (c_("q1", c) if "a" in opt["pe_init"] else c_(C, c, PO))
+                tt(out, c_(a, c), c_(C, c, PO), minus)
+            if pe3:
+                for P, x in ((R[3], "bt"), (R[0], "q1")):
+                    for c in two:
+                        mms([(c_(P, c, PO), S("idf"), c_(x, c), False, True)])
+            if last:
+                for c in two:
+                    if opt["pe_m"]:
+                        mm(c_(E, c, PO), S("jw"), c_(ab, c), S("nib"), c_(yw, c))
+                    else:
+                        tt(c_(E, c, PO), c_(ab, c), c_(E, c, PO), plus)
+                for c in two:
+                    tt(c_(ab, c), c_(yw, c, K), c_(E, c, PO), mul)
+            elif t > 0:
+                if opt["m_dma"]:
+                    for c in two:
+                        act(c_("xs", c), c_(E, c, PO))
+                    gdma(S(ab), S("xs"))
+                else:
+                    for c in two:
+                        tt(c_(ab, c), c_(ab, c), c_(E, c, PO), plus)
+        for P, v, new, on in ((R[3], vb, "bt", "b"), (R[2], "vaa", "q1", "a")) if not pe3 else ():
+            for c in two:
+                if on in opt["pe_init"]:
+                    mm(c_(P, c, PO), S("nif"), c_(new, c), S("idb"), c_(v, c))
+                else:
+                    tt(c_(P, c, PO), c_(v, c), c_(P, c, PO), minus)
+        for t in range(TV - 1, -1, -1):
+            a, b, yw, ab, ea, eb = "a%d" % t, bn[t], "yw%d" % t, "ab%d" % t, "ea%d" % t, "eb%d" % t
+            if t == 0 and not last:
+                win = S("dw", 0, O2)
+                for i, c in enumerate(three):
+                    act(c_("da", c), I(win, o_(ga[0], c)), scale=-1.0)
+                    if i > 0:
+                        act(c_("db", two[i - 1]), I(win, o_(gb[0], two[i - 1])), scale=-1.0)
+                for i, c in enumerate(three):
+                    tt(c_(R[0], c, PO), c_(R[0], c, PO), c_("da", c), mul)
+                    if i > 0:
+                        tt(c_("xs", two[i - 1]), c_(R[3], two[i - 1], PO), c_("db", two[i - 1]), mul)
+                for c in two:
+                    tt(c_("xs", c), c_(R[0], c, PO), c_("xs", c), plus)
+                for c in two:
+                    tt(c_(R[2], c, PO), c_(R[2], c, PO), c_(ls, c), plus)
+                for c in two:
+                    tt(c_("up", c), c_(R[2], c, PO), c_("xs", c), AluOpType.is_gt)
+                break
+            DA, DB, Q, Q2 = [(R[3], R[2], R[0], R[1]), (R[1], R[0], R[2], R[3]), (R[2], R[3], R[0], R[1])][t]
+            if pe3:
+                DA, DB, Q, Q2 = [(R[3], R[0], R[1], R[2]), (R[1], R[2], R[0], R[3]), (R[0], R[3], R[2], R[1])][t]
+            aa, bb = "aa%d" % (t % 2), "bb%d" % (t % 2)
+            if not last:
+                act(S(aa), S(a), Square)
+                act(S(bb), S(b), Square)
+            elif t != 1:
+                coef(aa, a, Q, yw)
+                coef(bb, b, Q2, yw)
+            if t < 2:
+                win = S("dw", 0, O1 if t == 1 else O2)
+                for c in two:
+                    for d, D, lst in (("da", DA, ga[t]), ("db", DB, gb[t])):
+                        act(c_(d, c), I(win, o_(lst, c)))
+                        if d in opt["pe_cp"]:
+                            mm(c_(D, c, PO), S("idf"), c_(d, c))
+                        else:
+                            act(c_(D, c, PO), c_(d, c))
+            base = O0 + 2 * K * (2 - t)
+
+            def terms():
+                if t == 2:
+                    for c in wide:
+                        tt(c_("pa", c), c_(eb, c), c_(DA, c, PO), mul)
+                        tt(c_("pb", c), c_(ea, c), c_(DB, c, PO), mul)
+                    send([([S("pa"), S("pb")], -2 * STEP, S(lu))], relay=True)
+                    return
+                u = "u1" if t == 1 else "lu1"
+                for c in two:
+                    if opt["fuse"]:
+                        tt(c_(u, c), I(win, o_(gb[t], c)), c_(ea, c), mul)
+                    else:
+                        tt(c_(u, c), c_(ea, c), c_(DB, c, PO), mul)
+                if t == 1:
+                    for c in two:
+                        tt(c_("q1", c), c_(eb, c), c_(DA, c, PO), mul)
+                    send([([S("u1"), S("q1")], -STEP, S(ls))], relay=True)
+                    return
+                for c in two:
+                    tt(c_(Q2, c, PO), c_(eb, c), c_(DA, c, PO), mul)
+                    tt(c_("da", c), c_(Q2, c, PO), c_(u, c), plus)
+                gdma(S(lu), S(ls))
+                gdma(S("da", 0, K), S(lu))
+                act(S("pa"), I(S("da", 0, K), S("pos")), scale=0.125)
+                dma(lambda T: T.yh[:], lambda T: T.pa[:], [S("pa")], [], 500e3)
+
+            def side(sq, D1, D2, P, t1, out, base, cs):
+                for c in cs:
+                    tt(c_(t1, c), c_(sq, c), c_(D1, c, PO), mul)
+                    tt(c_(P, c, PO), c_(ab, c), c_(D2, c, PO), mul)
+                if last:
+                    for c in cs:
+                        tt(c_(out, c, base), c_(t1, c), c_(P, c, PO), minus)
+                    return
+                for c in wide:
+                    tt(c_(P, c, PO), c_(t1, c), c_(P, c, PO), plus)
+                for c in wide:
+                    tt(c_(t1, c), c_(yw, c, K), c_(P, c, PO), mul)
+                for c in wide:
+                    tt(c_(out, c, base), c_(D1, c, PO), c_(t1, c), minus)
+
+            if t < 2:
+                terms()
+            side(aa, DB, DA, Q, "xs", *(("dw", base + K) if k == 0 else ("bt", 0)), two)
+            back("dw", base + K, t)
+            side(bb, DA, DB, Q2, "da" if t == 1 else "q1" if t == 2 else "ls1", "dw", base, wide)
+            if t == 2:
+                if last:
+                    coef("aa1", "a1", Q, "yw1")
+                    coef("bb1", "b1", Q2, "yw1")
+                terms()
+            if t == 1 and not last:
+                for P, x in ((R[0], "eb0"), (R[3], "ea0"), (R[2], lu)):
+                    for c in two:
+                        mm(c_(P, c, PO), S("idf"), c_(x, c))
+                for c in two:
+                    mms([(c_(R[1], c, PO), S("bm"), S("one"), True, False)])
+        if last:
+            for c in range(2):
+                out, src = S("wf", c * W // 2, (c + 1) * W // 2), I(S("dw", 0, O2 + 2 * K), S("hl", c * 64, (c + 1) * 64))
+                if c == 0:
+                    ts(out, src, -1.0, mul)
+                else:
+                    act(out, src, scale=-1.0)
+                dma(lambda T, c=c: T.yd[:, c * W // 2:(c + 1) * W // 2], lambda T, c=c: T.wf[:, c * W // 2:(c + 1) * W // 2],
+                    [out], [], 520e3)
+            break
+        Z = R[1]; n = k + 1; lw = "lw%d" % n
+        mms([(S(Z, PO + s * KW, PO + (s + 1) * KW), S("vm"), ("up", s, K, 16), False, s % 8 == 7) for s in range(16)])
+        scan(S("db"), S(Z, PO, PO + K), S("kr"), -1.0)
+        ts(S("da", 0, 1), S("db", K - 1), -JM * 1024, plus)
+        scan(S("da", 1, K + 1), S(Z, PO, PO + K), S("kr"), S("da", 0, 1))
+        for lists, grp in (([5], "p%d" % n), ([0], "i%d" % n), ([1, 2, 3, 4], "o%d" % n)):
+            for i in lists:
+                wrap(S("wp", i * KW, (i + 1) * KW), S("da", 0, K), rows[i], grp)
+                wrap(S("wc", i * KW, (i + 1) * KW), S("da", 1, K + 1), rows[i], grp)
+            lo, hi = lists[0] * KW, (lists[-1] + 1) * KW
+            tt(S("wp", lo, hi), S("wp", lo, hi), S("wc", lo, hi), minus)
+            tt(S("br", lo, hi), S("wp", lo, hi), S("kw", lo, hi), plus)
+            ts(S("br", 400 + lo, 400 + hi), S("br", lo, hi), int(JM) - 1, AluOpType.bitwise_and)
+            cp(S(lw, lo, hi), S("br", 400 + lo, 400 + hi))
+        send([([S(lw, 2 * KW, 4 * KW)], STEP, S("v1%d" % n)), ([S(lw, 4 * KW)], 2 * STEP, S("v2%d" % n))], also=[S(lu), S(ls)])
+        act(I(S("q1"), S(lw, 0, KW)), S("vj"), Silu)
+        wrap(S("iw"), S("q1"), 0)
+        tolist(S("x0%d" % n), S("iw"), O0 + K)
+        send([([S("x0%d" % n)], STEP, S("x1%d" % n)), ([S("x0%d" % n)], 2 * STEP, S("x2%d" % n))])
+        if n < RO - 1:
+            tt(S("kw"), S("br", 400, 400 + 6 * KW), S("j6"), plus)
+            for i in range(6):
+                unwrap(S("kr"), rows[i], S("kw", i * KW, (i + 1) * KW), "unk%d" % n)
+    mem = {}
+    for i, o in enumerate(ops):
+        if o["group"] is not None:
+            mem.setdefault(o["group"], []).append(i)
+    for o in ops:
+        full = set()
+        for j in o["deps"]:
+            full.update(mem[ops[j]["group"]] if ops[j]["group"] is not None else [j])
+        o["deps"] = sorted(full)
+    return ops, sems, mem, relays
+
+
+def times(ops, m):
+    cost = [o["cost"](m) for o in ops]
+    lat = [o["lat"](m) if o["lat"] else 0.0 for o in ops]
+    gap = [0.0 if o["kind"] == "r" else m["hop"] for o in ops]
+    return cost, lat, gap
+
+
+def replay(ops, seq, tm):
+    cost, lat, gap = tm
+    free, st, fin = {}, [0.0] * len(ops), [0.0] * len(ops)
+    for i in seq:
+        o = ops[i]; s = free.get(o["q"], 0.0)
+        for d in o["deps"]:
+            if fin[d] + gap[i] > s:
+                s = fin[d] + gap[i]
+        if o["q"] != "-":
+            free[o["q"]] = s + cost[i]
+        st[i] = s; fin[i] = s + cost[i] + lat[i]
+    return st, fin
+
+
+def place(ops, key, tm):
+    cost, lat, gap = tm
+    n = len(ops); busy, st, fin = {}, [0.0] * n, [0.0] * n
+    turn = sorted(range(n), key=lambda i: (key[i], i))
+    for i in turn:
+        o = ops[i]; s = 0.0
+        for d in o["deps"]:
+            if fin[d] + gap[i] > s:
+                s = fin[d] + gap[i]
+        if o["q"] != "-":
+            line = busy.setdefault(o["q"], []); p = len(line)
+            while p > 0 and line[p - 1][1] > s:
+                p -= 1
+            while p < len(line) and line[p][0] < s + cost[i]:
+                s = max(s, line[p][1]); p += 1
+            line.insert(p, (s, s + cost[i]))
+        st[i] = s; fin[i] = s + cost[i] + lat[i]
+    return sorted(turn, key=lambda i: st[i])
+
+
+def order(ops, tries, seed=1):
+    tms = [times(ops, m) for m in SPREAD]; rng = np.random.default_rng(seed); n = len(ops)
+    best = None; own = [float(i) if o["main"] else float(n + i) for i, o in enumerate(ops)]
+    for it in range(tries):
+        new = list(own if best is None else best[2])
+        if best is not None:
+            for j in rng.integers(0, n, 1 + it % 3):
+                new[j] = best[3][j] + float(rng.normal()) * (3.0, 10.0, 40.0)[it % 3]
+        key = list(new)
+        for i in range(n - 1, -1, -1):
+            for d in ops[i]["deps"]:
+                if key[i] < key[d]:
+                    key[d] = key[i]
+        seq = place(ops, key, tms[0])
+        first = max(replay(ops, seq, tms[0])[1])
+        if best is not None and first > best[4] + 1.5:
+            continue
+        val = first + sum(max(replay(ops, seq, tm)[1]) for tm in tms[1:])
+        if best is None or val <= best[0]:
+            best = (val, seq, new, key, first)
+    return best[1]
+
+
+OPS, SEMAPHORES, MEM, RELAYS = build(OPT)
+SEQ = order(OPS, TRIES)
+
+
+def rank_program(g, core, T, topo):
+    rank = T.rank_of(core)
+    if rank is None:
+        served = [r for r, c in enumerate(T.cores) if topo.chip(c) == topo.chip(core) and helper(T, topo, c) == core]
+        sent = 0
+        for i, step, hold, land in sorted(RELAYS, key=lambda x: SEQ.index(x[0])) if served else []:
+            dst = T.cores[(served[0] + step) % N]; rid, pid, _ = topo.addr(dst); n = OPS[i]["cnt"] // 2
+            g.wait_ge(T.sem["h%d" % i], n)
+            g.remote_dma(ap(T, land), ap(T, hold), T.sem["a%d_%d" % (i, step % N)], T.sem.hand, pid, rid,
+                         sum(1 << e for e in topo.engines(core, dst)[:n]))
+            sent += n
+        if sent:
+            g.wait_ge(T.sem.hand, sent)
+        return
+    ctx = dict(rank=rank, core=core, topo=topo)
+    queue = {"v": g.vector, "s": g.scalar, "t": g.tensor, "g": g, "y": g.sync}
+    count, mark, seen, top = {}, {}, {}, {}
+    for i in SEQ:
+        o = OPS[i]
+        if o["kind"] == "c":
+            sem = "c" + o["q"]; count[sem] = count.get(sem, 0) + 1
+            mark[i] = (sem, count[sem])
+        else:
+            mark[i] = (o["group"], sum(OPS[j]["cnt"] for j in MEM[o["group"]]))
+            count[o["group"]] = mark[i][1]
+        if o["kind"] == "r":
+            continue
+        need = {}
+        for j in o["deps"]:
+            sem, v = mark[j]
+            need[sem] = max(need.get(sem, 0), v)
+        for sem, v in sorted(need.items()):
+            if seen.get((o["q"], sem), 0) < v:
+                queue[o["q"]].wait_ge(T.sem[sem], v)
+                seen[(o["q"], sem)] = v; top[sem] = max(top.get(sem, 0), v)
+        ins = o["fn"](g, T, ctx)
+        if o["kind"] == "c":
+            ins.then_inc(T.sem[mark[i][0]], 1)
+        elif o["kind"] == "d":
+            ins.then_inc(T.sem[o["group"]], 16)
+    for sem, v in sorted(count.items()):
+        if top.get(sem, 0) < v:
+            g.wait_ge(T.sem[sem], v)

@@ -6,12 +6,13 @@ N, W, K, TV, STEP, RO = 8, 2048, 960, 3, 3, 3
 H = K // 2
 KW = K // 16
 O0, O1, O2 = W, W + 2 * K, W + 4 * K
-FAR = 10240
 JM = 8192.0
+LOW = -1024 * JM
 PO = 32
-OPT = dict(m_dma=True, pe_e=True, pe_init="ab", pe_m=True, pe3=True, fuse=True, put="sssvss", get="svvssvsvsssss", pe_cp="",
-           full=True, head=160, relay=False)
-TRIES = 14000
+OPT = dict(m_dma="12", put="sssvss", get="svvssvsvsssss", head=160, pa0="", fd="", mid2="ab", mid1="",
+           ord2="batBA", ord1="uqtbBaA", ord3=["uqtba", "uqtba", "tba"], fin=["", "", ""], outs="vs",
+           wide="w t2 cm cf".split(), half=[], own=dict(y=1, t2=1, t1=2))
+TRIES = 12000
 F32, BF, I32, U16 = "float32", "bfloat16", "int32", "uint16"
 
 SCRATCH = {}
@@ -27,12 +28,12 @@ for _n, _c, _d in [
         ("vaa", K, BF), ("vbs", K, BF), ("vbb", K, BF), ("kr", K, F32), ("br", K, I32), ("up", K, BF),
         ("ani", 3 * KW, I32), ("bri", KW, I32), ("n0", 2 * KW, U16), ("nb0", KW, U16), ("s1", 2 * KW, U16),
         ("s2", 2 * KW, U16), ("r1", 2 * KW, U16), ("r2", 2 * KW, U16),
-        ("ia", 128, I32), ("fa", 128, F32), ("fb", 128, F32),
+        ("ia", 128, I32), ("fa", 128, F32), ("hot", 16, F32), ("end", 16, F32),
         ("pi", 8, I32), ("pj", 8, I32), ("pf", 8, F32), ("cw", 128, F32), ("jw", 128, F32), ("j6", 6 * KW, F32),
-        ("rho", KW, U16), ("pos", KW, U16), ("rh2", 128, U16), ("po2", 128, U16), ("sw2", 128, F32),
+        ("rho", KW, U16), ("pos", KW, U16), ("rh2", 128, U16), ("po2", 128, U16),
         ("dl", 128, U16), ("hl", 128, U16), ("gw", 2 * KW, F32),
         ("f1", 2 * KW, U16), ("f2", 2 * KW, U16), ("g1", 2 * KW, U16), ("g0", 2 * KW, U16), ("home", 3 * KW, U16),
-        ("kw", 6 * KW, F32), ("wp", 384, F32), ("wc", 6 * KW, F32), ("iw", KW, F32),
+        ("kw", 6 * KW, F32), ("wp", 384, F32), ("wc", 384, F32), ("iw", KW, F32),
         ("lw1", 6 * KW, U16), ("lw2", 6 * KW, U16), ("v11", 2 * KW, U16), ("v12", 2 * KW, U16),
         ("v21", 2 * KW, U16), ("v22", 2 * KW, U16), ("x01", KW, U16), ("x02", KW, U16), ("x11", KW, U16),
         ("x12", KW, U16), ("x21", KW, U16), ("x22", KW, U16),
@@ -43,8 +44,10 @@ for _i in range(4):
     SCRATCH["ps%d" % _i] = ("psum", [128, 1024], F32)
 SIZE = {F32: 4, BF: 2, I32: 4, U16: 2}
 
-NOM = dict(cyc=0.00102, gat=1.5, sca=3.5, fix=0.06, hop=0.12, pe=0.0005, dma=2.1, gdma=1.0, rem=1.2, net=2.5, bw=70e3)
-SPREAD = [NOM, dict(NOM, gat=1.1, sca=2.0), dict(NOM, gat=2.0, sca=5.5), dict(NOM, dma=3.0, net=4.0, bw=45e3, pe=0.0007)]
+NOM = dict(cyc=0.00102, gat=1.5, sca=3.5, fix=0.06, hop=0.12, pe=0.0005, dma=2.1, gdma=1.0, rem=1.2, net=2.5, bw=70e3,
+           acc=300e3, blk=0.3)
+SPREAD = [NOM, dict(NOM, gat=1.1, sca=2.0, cyc=0.0009), dict(NOM, gat=2.0, sca=5.5),
+          dict(NOM, dma=3.0, net=4.0, bw=45e3, pe=0.0007, acc=200e3, blk=0.6)]
 
 
 def S(name, lo=0, hi=None):
@@ -163,9 +166,8 @@ def build(opt):
         return add("v", lambda g, T, c: g.vector.memset(ap(T, out), v), [], [out], ecost(out, [], 1))
 
     def scan(out, d0, d1, init):
-        col = [init] if isinstance(init, tuple) else []
-        return add("v", lambda g, T, c: g.vector.tensor_tensor_scan(ap(T, out), ap(T, d0), ap(T, d1), ap(T, init) if col else init,
-                                                                    AluOpType.max, AluOpType.min), [d0, d1] + col, [out], ecost(out, [d0], 1))
+        return add("v", lambda g, T, c: g.vector.tensor_tensor_scan(ap(T, out), ap(T, d0), ap(T, d1), init, AluOpType.max, AluOpType.min),
+                   [d0, d1], [out], ecost(out, [d0], 1))
 
     def act(out, x, func=ActivationFunctionType.Copy, scale=None, bias=None):
         def fn(g, T, c):
@@ -185,11 +187,6 @@ def build(opt):
             return ins
         return add("t", fn, [x for p in parts for x in p[1:3]], [p[0] for p in parts], lambda m: 0.03 * len(parts) + n * m["pe"])
 
-    def mm(out, lhs, rhs, *more):
-        if more:
-            return mms([(out, lhs, rhs, True, False), (out, more[0], more[1], False, True)])
-        return mms([(out, lhs, rhs, True, True)])
-
     def iota(out, pat, base, cm):
         fl = SCRATCH[out[0]][2] != I32
 
@@ -205,30 +202,33 @@ def build(opt):
     def dma(fo, fi, reads, writes, nb, group=None, q="y"):
         def fn(g, T, c):
             return (g.sync if q == "y" else g.scalar).dma_start(fo(T), fi(T))
-        return add(q, fn, reads, writes, lambda m: 0.1, "d", lambda m: m["dma"] + nb / 500e3, group)
+        big = nb > 250e3
+        return add(q, fn, reads, writes, lambda m: 0.1, "d",
+                   lambda m: [(m["dma"] - 1.0, "E", nb / 600e3 if big else 0.05, 1.0 if big else 1.0 + nb / 600e3)], group)
 
     def gdma(out, src, acc=True):
         def fn(g, T, c):
             if acc:
                 return g.dma_start(ap(T, out), ap(T, src), accum_op=AluOpType.add)
             return g.dma_start(ap(T, out), ap(T, src))
-        return add("g", fn, [src, out] if acc else [src], [out], lambda m: m["gdma"], "d", lambda m: m["dma"] + width(out) * 512 / 300e3)
+        return add("g", fn, [src, out] if acc else [src], [out], lambda m: m["gdma"], "d",
+                   lambda m: [(m["dma"] - 1.0, "E", width(out) * 512 / m["acc"], 1.0)])
 
-    def wrap(out, src, row, group=None):
-        return dma(lambda T: ap(T, out), lambda T: T[src[0]][row::16, src[1]:src[2]], [src], [out], 200e3, group)
+    def wrap(out, src, row, group=None, q="y"):
+        return dma(lambda T: ap(T, out), lambda T: T[src[0]][row::16, src[1]:src[2]], [src], [out], 200e3, group, q)
 
     def unwrap(out, row, src, group=None):
         return dma(lambda T: T[out[0]][row::16, out[1]:out[2]], lambda T: ap(T, src), [src], [out], 200e3, group)
 
-    def send(parts, also=(), relay=False):
+    def send(parts, also=(), own=0):
         i = len(ops); hand = None
-        if relay and opt["relay"]:
+        if own:
             (srcs, step, land), = parts
-            h = (land[2] - land[1]) // 2
-            parts = [([S(x[0], x[1], x[1] + h) for x in srcs], step, S(land[0], land[1], land[1] + h))]
-            upper = S(land[0], land[1] + h, land[2])
-            hold = upper if land[0].startswith("yw") else S("dw", len(relays) * h, (len(relays) + 1) * h)
-            hand = [S(x[0], x[1] + h, x[2]) for x in srcs]
+            h = (land[2] - land[1]) // (own + 1)
+            parts = [([S(x[0], x[1] + j * h, x[1] + (j + 1) * h) for x in srcs], step, S(land[0], land[1] + j * h, land[1] + (j + 1) * h))
+                     for j in range(own + 1)]
+            hand, _, upper = parts.pop()
+            hold = upper if land[0].startswith("yw") else S("dw", len(relays) * H, len(relays) * H + h)
             relays.append((i, step, hold, upper)); sems.append("h%d" % i)
         per = 8 // (1 << (len(parts) - 1).bit_length())
         names = {}
@@ -243,16 +243,17 @@ def build(opt):
                 tr.append(transfer(c["topo"], dst, mask, T.sem["a%d_%d" % (i, step % N)], [ap(T, s) for s in srcs], ap(T, land)))
             if hand:
                 by = helper(T, c["topo"], c["core"])
-                eng = [e for e in c["topo"].engines(c["core"], by) if not used >> e & 1][:per]
+                eng = [e for e in c["topo"].engines(c["core"], by) if not used >> e & 1][:8]
                 tr.append(transfer(c["topo"], by, sum(1 << e for e in eng), T.sem["h%d" % i], [ap(T, s) for s in hand], ap(T, hold)))
             return g.remote_dma_fused(tr, local_sem=T.sem["d%d" % i])
         nb = sum(128 * width(p[0][0]) * SIZE[SCRATCH[p[0][0][0]][2]] for p in parts)
         add("g", fn, [s for p in parts for s in p[0]] + (hand or []), list(also), lambda m: m["rem"], "x",
-            lambda m: 1.0 + nb / m["bw"], cnt=per * len(parts) * (2 if hand else 1))
+            lambda m: [(1.0, "E", 0.3 + m["blk"] * 2 * nb / m["bw"], 0.0), (1.0, "L", 2 * nb / m["bw"], 0.0)]
+            + ([(1.0 + nb / own / 100e3 + m["net"] + m["rem"], "M", 2 * nb / own / m["bw"], -1.0)] if hand else []),
+            cnt=per * len(parts) + (8 if hand else 0))
         for step, lands in names.items():
-            add("-", None, [], lands + ([upper] if hand else []), lambda m: 0.0, "r",
-                lambda m: m["net"] - 1.0 + (2.0 + m["rem"] + nb / 200e3 if hand else 0.0), "a%d_%d" % (i, step % N),
-                after=[i], cnt=per * len(lands) * (2 if hand else 1))
+            add("-", None, [], lands + ([upper] if hand else []), lambda m: 0.0, "r", lambda m: [(m["net"] - 1.0, "", 0.0, 0.0)],
+                "a%d_%d" % (i, step % N), after=[i], cnt=per * len(lands) + (8 if hand else 0))
 
     mul, plus, minus, mx = AluOpType.mult, AluOpType.add, AluOpType.subtract, AluOpType.max
     Silu, Square, Ident = ActivationFunctionType.Silu, ActivationFunctionType.Square, ActivationFunctionType.Identity
@@ -271,10 +272,10 @@ def build(opt):
     dma(lambda T: T.bri[:], lambda T: T.bn[0::TV, :], [], [S("bri")], 200e3, "names")
     for t in range(TV):
         dma(lambda T, t=t: T.br[4 * t::16, :], lambda T, t=t: T.bn[t::TV, :], [], [S("br")], 100e3, "rows")
+    dma(lambda T: T.raw[:, :K], lambda T: T.yt[:], [], [S("raw", 0, K)], 260e3, q="s")
     dma(lambda T: T.thb[:], lambda T: T.th[:], [], [S("thb")], 520e3, q="s")
-    dma(lambda T: T.raw[:, :K], lambda T: T.yt[:], [], [S("raw", 0, K)], 500e3, q="s")
-    dma(lambda T: T.raw[:, K:], lambda T: T.wt[:], [], [S("raw", K)], 500e3, q="s")
-    dma(lambda T: T.vab[:], lambda T: T.va[:], [], [S("vab")], 900e3)
+    dma(lambda T: T.raw[:, K:], lambda T: T.wt[:], [], [S("raw", K)], 260e3, q="s")
+    dma(lambda T: T.vab[:], lambda T: T.va[:], [], [S("vab")], 520e3)
     iota(S("pi", 0, 1), [[0, 1]], 0, 1)
     iota(S("cw"), [[16, 128]], 0, 0)
     iota(S("jw"), [[1, 128]], 0, 0)
@@ -301,12 +302,13 @@ def build(opt):
     cp(S("nb0"), S("wp", 0, KW))
     send([([S("s1")], STEP, S("r1")), ([S("s2")], 2 * STEP, S("r2"))])
     who = {k: list(opt[k]) for k in ("put", "get")}
+    wa, wb = S("wf"), S("dw", O2)
 
-    def put(lst, val):
+    def put(table, lst, val):
         if who["put"].pop(0) == "v":
-            cp(I(S("wf"), lst), val)
+            cp(I(table, lst), val)
         else:
-            act(I(S("wf"), lst), val, Silu)
+            act(I(table, lst), val, Silu)
 
     def get(out, src, f=1.0):
         if who["get"].pop(0) == "v":
@@ -314,47 +316,48 @@ def build(opt):
         else:
             act(out, src, scale=f)
 
-    put(S("n0", 0, KW), S("dw", O0, O0 + K))
-    put(S("n0", KW), S("vj"))
+    put(wa, S("n0", 0, KW), S("dw", O0, O0 + K))
+    put(wa, S("n0", KW), S("vj"))
     sw0, sw1, l2, l1, lh = S("wc", 0, 128), S("wc", 128, 256), S("wp", 0, 128), S("wp", 128, 256), S("wp", 256, 384)
-    wrap(sw0, S("wf"), 0)
+    wrap(sw0, wa, 0)
     get(S("yw0", 0, K), I(S("raw", 0, K), S("rho")))
     get(S("b0"), I(S("thb"), S("n0", 0, KW)))
     get(S("a0"), I(S("b0"), S("rho")))
     get(S("yw0", K), I(S("raw", K), S("rho")), 0.125)
     get(S("b0s"), I(S("thb"), S("n0", KW)))
-    send([([S("yw0")], STEP, S("yw1"))], relay=True)
-    send([([S("yw0")], 2 * STEP, S("yw2"))], relay=True)
+    send([([S("yw0")], STEP, S("yw1"))], own=opt["own"]["y"])
+    send([([S("yw0")], 2 * STEP, S("yw2"))], own=opt["own"]["y"])
     gdma(S("tw", 0, W), S("thb"), False)
     fill(S("onf"), 1.0)
     keep(S("idf"), S("onf"), [[-1, 128]], AluOpType.is_equal, 0, 1)
     cp(S("idb"), S("idf"))
-    if opt["pe_e"] or opt["pe_m"]:
-        ts(S("nib"), S("idf"), -1.0, mul)
-    if opt["pe_init"] or opt["pe3"]:
-        ts(S("nif"), S("idf"), -1.0, mul)
-    for lo in range(O1, O2 + 2 * K, K):
-        iota(S("dw", lo, lo + K), [[1, 16], [16, KW]], lo if lo < O2 else lo - O2 + FAR, 0)
+    ts(S("nib"), S("idf"), -1.0, mul)
+    ts(S("nif"), S("idf"), -1.0, mul)
+    for lo in (O1, O1 + K, O0 + K):
+        iota(S("dw", lo, lo + K), [[1, 16], [16, KW]], lo, 0)
+    iota(S("dw", O2, O2 + 512), [[1, 4], [16, 128]], 0, 0)
+    act(S("dw", O2 + 512, O2 + 1024), S("dw", O2, O2 + 512), Ident, 1.0, 4.0)
+    act(S("dw", O2 + 1024), S("dw", O2, O2 + 1024), Ident, 1.0, 8.0)
     ta = [S("n0", 0, KW), S("r1", 0, KW), S("r2", 0, KW)]
     tb = [S("nb0"), S("r1", KW), S("r2", KW)]
 
-    def lookup(out, t, row):
-        get(S("lu1"), I(S("wf"), ta[t]))
-        wrap(S("gw", 0, KW), S("lu1"), row)
-        tolist(S(out, 0, KW), S("gw", 0, KW))
-        get(S("ls1"), I(S("wf"), tb[t]))
-        wrap(S("gw", KW), S("ls1"), row)
-        tolist(S(out, KW), S("gw", KW))
+    def lookup(out, table, t, row, via=("lu1", "ls1", S("gw"))):
+        for i, lst in enumerate((ta[t], tb[t])):
+            cut = S(via[2][0], via[2][1] + i * KW, via[2][1] + (i + 1) * KW)
+            get(S(via[i]), I(table, lst))
+            wrap(cut, S(via[i]), row)
+            tolist(S(out, i * KW, (i + 1) * KW), cut)
 
-    lookup("f1", 1, 0)
-    put(ta[1], S("dw", O1, O1 + K))
-    put(tb[1], S("dw", O1 + K, O2))
-    wrap(sw1, S("wf"), 0)
-    lookup("f2", 2, 0)
+    lookup("f1", wa, 1, 0)
+    put(wa, ta[1], S("dw", O1, O1 + K))
+    put(wa, tb[1], S("dw", O1 + K, O2))
+    wrap(sw1, wa, 0)
+    lookup("f2", wa, 2, 0)
     tolist(S("dl"), sw1)
-    put(ta[2], S("dw", O2, O2 + K))
-    put(tb[2], S("dw", O2 + K, O2 + 2 * K))
-    wrap(S("sw2"), S("wf"), 0)
+    put(wb, ta[2], S("dw", O0, O0 + K))
+    put(wb, tb[2], S("dw", O0 + K, O1))
+    wrap(l2, wb, 0)
+    lookup("g1", wb, 1, 0, ("pa", "pb", S("wc", 256)))
     act(S("raw"), I(S("vab"), S("r2")))
     act(S("vaa"), I(S("raw", 0, K), S("rho")))
     act(S("vbs"), I(S("raw", K), S("rho")))
@@ -368,18 +371,15 @@ def build(opt):
         tt(S("fa"), S("fa"), sw, AluOpType.min)
         tt(out, below, S("fa"), mx)
 
-    ts(S("sw2"), S("sw2"), float(O0 - FAR), plus)
-    tt(l2, S("cw"), S("sw2"), mx)
     overlay(l1, l2, sw1, O1, O1)
     overlay(lh, l1, sw0, O0, O2)
-    for row, src in ((0, l2), (4, l1), (8, lh)):
-        unwrap(S("wf"), row, src, "unl")
-    lookup("g1", 1, 0)
-    lookup("g0", 0, 4)
+    for row, src in ((4, l1), (8, lh)):
+        unwrap(wa, row, src, "unl")
+    lookup("g0", wa, 0, 4)
     places(S("po2"), 128)
-    act(S("dw", O2), I(S("wf"), S("po2")))
-    wrap(S("sw2"), S("dw", O2), 8)
-    tolist(S("hl"), S("sw2"))
+    act(wb, I(wa, S("po2")))
+    wrap(sw0, wb, 8)
+    tolist(S("hl"), sw0)
     send([([S("f1", KW)], -STEP, S("home", 0, KW)), ([S("g1", KW)], -STEP, S("home", KW, 2 * KW)),
           ([S("f2", KW)], -2 * STEP, S("home", 2 * KW))])
     rows = [4, 8, 12, 2, 6, 0]
@@ -400,8 +400,10 @@ def build(opt):
     keep(S("vm"), S("vm"), [[-16, 8], [0, 16]], AluOpType.is_ge, 0, 1)
     keep(S("vm"), S("vm"), [[16, 8], [0, 16]], AluOpType.is_gt, 32, -1)
     add("v", lambda g, T, c: g.vector.memset(T.vm[0:16, 112:128], 2.0 ** 25), [], [S("vm", 112)], lambda m: 0.13)
-    if opt["pe_m"]:
-        ts(S("jw"), S("idf"), 2.0, mul)
+    keep(S("onf"), S("onf"), [[-16, 8], [0, 16]], AluOpType.is_ge, 0, 1)
+    keep(S("onf"), S("onf"), [[16, 8], [0, 16]], AluOpType.is_gt, 16, -1)
+    ts(S("hot"), S("jw", 0, 16), S("pf", 0, 1), AluOpType.is_equal)
+    ts(S("jw"), S("idf"), -2.0, mul)
 
     def c_(name, c, base=0):
         return S(name, base + c[0], base + c[1])
@@ -409,15 +411,34 @@ def build(opt):
     def o_(x, c):
         return S(x[0], x[1] + c[0] // 16, x[1] + c[1] // 16)
 
-    def coef(sq, x, P, yw):
-        act(S(P, PO, PO + K), S(x), Square)
-        tt(S(sq), S(yw, K), S(P, PO, PO + K), mul)
-        act(S(sq), S(sq), Ident, -1.0, 1.0)
-
     main[0] = True
     two = [(0, H), (H, K)]
-    wide = [(0, K)] if opt["full"] else two
     three = [(0, opt["head"]), (opt["head"], H), (H, K)]
+
+    def vv(name, out, x, y, op):
+        def at(v, c):
+            if isinstance(v, str):
+                return c_(v, c, PO if v.startswith("ps") else 0)
+            return I(v[0], o_(v[1], c)) if isinstance(v[0], tuple) else c_(v[0], c, v[1])
+        for c in [(0, K)] if name in opt["wide"] else two:
+            tt(at(out, c), at(x, c), at(y, c), op)
+
+    def pe(P, *terms):
+        for c in two:
+            mms([(c_(P, c, PO), S(mat), S("one") if x == "one" else c_(x, c, lo), i == 0, i == len(terms) - 1)
+                 for i, (mat, x, lo) in enumerate(terms)])
+
+    def adds(name, out, src):
+        out = (out, 0) if isinstance(out, str) else out
+        for c in two if name in opt["half"] else [(0, K)]:
+            gdma(c_(out[0], c, out[1]), c_(src, c))
+
+    def square(out, x):
+        act(S(out, PO, PO + K) if out.startswith("ps") else S(out, 0, K), S(x), Square)
+
+    def picks(name, out, win, lst, cs):
+        for c in [(0, K)] if name in opt["wide"] else cs:
+            act(c_(out, c), I(win, o_(lst, c)))
 
     for k in range(RO):
         last = k == RO - 1
@@ -430,6 +451,7 @@ def build(opt):
         bn = ["b0s" if k == 0 else "b0", "b1", "b2"]
         vb = "vbs" if k == 0 else "vbb"
         lu, ls = "lu%d" % (k % 2), "ls%d" % (k % 2)
+        cof = [("aa0", "bb0"), ("aa1", "bb1"), ("u1", "db")]
 
         def back(win, base, t):
             if k > 0:
@@ -438,20 +460,15 @@ def build(opt):
         for t in range(TV):
             E, C, X = R[1 if t != 1 else 0], R[2], R[3]
             a, b, yw, ab, ea, eb = "a%d" % t, bn[t], "yw%d" % t, "ab%d" % t, "ea%d" % t, "eb%d" % t
-            pe3 = last and t == 2 and opt["pe3"]
-            for c in two:
-                if not opt["pe_e"]:
-                    mm(c_(E, c, PO), S("idb"), c_(yw, c))
-                mm(c_(C, c, PO), S("idb"), c_(yw, c, K))
+            pe3 = last and t == 2
+            pe(C, ("nib", yw, K))
             if t == 0:
                 win, lst = (S("thb"), S("n0", KW)) if k == 0 else (S("b0s"), S("lw%d" % k, 5 * KW))
             else:
                 win, lst = S("tw", 0, O1 if t == 1 else O2), fb[t]
-                for c in three:
-                    act(c_(a, c), I(win, o_(fa[t], c)))
+                picks("", a, win, fa[t], three)
             if t > 0 or k > 0:
-                for c in two:
-                    act(c_(b, c), I(win, o_(lst, c)))
+                picks("fb", b, win, lst, two)
             if t == 2:
                 if k == 0:
                     act(S("thb"), I(S("vab"), S("rh2")))
@@ -460,181 +477,226 @@ def build(opt):
                 if k > 0:
                     act(S("vbb"), I(S("vbs"), S("v2%d" % k, KW)))
             base = O0 + 2 * K * t
-            for c in (three if t > 0 else two):
-                tt(c_(ab, c), I(win, o_(lst, c)), c_(a, c), mul)
-            for c in two:
-                if opt["pe_e"]:
-                    mm(c_(E, c, PO), S("idf"), c_(ab, c), S("nib"), c_(yw, c))
-                else:
-                    tt(c_(E, c, PO), c_(ab, c), c_(E, c, PO), minus)
-            for c in two:
-                tt(c_(ea, c), c_(E, c, PO), c_(a, c), mul)
+            if t == 0 and str(k) in opt["pa0"]:
+                pe(R[0], ("idb", a, 0))
+                vv("", ab, b, R[0], mul)
+            else:
+                for c in (three if t > 0 else two):
+                    tt(c_(ab, c), I(win, o_(lst, c)), c_(a, c), mul)
+            pe(E, ("idf", ab, 0), ("nib", yw, 0))
+            vv("ea", ea, E, a, mul)
             if pe3:
                 for P, v, x in ((R[3], vb, b), (R[0], "vaa", a)):
                     for c in two:
                         mms([(c_(P, c, PO), S("idb"), c_(v, c), True, False), (c_(P, c, PO), S("nif"), c_(x, c), False, False)])
-            for c in two:
-                tt(c_("bt", c) if pe3 else c_(X, c, PO), c_(ea, c), c_(C, c, PO), mul)
-            for c in two if not pe3 else ():
-                if t == 2:
-                    out = c_("bt", c) if "b" in opt["pe_init"] else c_(X, c, PO)
-                else:
-                    out = c_("tw", c, base + K) if k == 0 else c_("bt", c)
-                tt(out, c_(b, c), c_(X, c, PO), minus)
+            if pe3 or (last and "b" in opt["fd"]):
+                vv("tb", "bt", ea, C, mul)
+                if not pe3:
+                    adds("fb", "bt", b)
+            else:
+                vv("tb", X, ea, C, mul)
+                vv("bn", ("tw", base + K) if k == 0 and t < 2 else "bt", b, X, plus)
             if t < 2:
                 back("tw", base + K, t)
-            for c in two:
-                tt(c_(eb, c), c_(E, c, PO), c_(b, c), mul)
-            for c in two:
-                tt(c_("q1", c) if pe3 else c_(C, c, PO), c_(eb, c), c_(C, c, PO), mul)
-            for c in two if not pe3 else ():
-                out = c_("tw", c, base) if t < 2 else (c_("q1", c) if "a" in opt["pe_init"] else c_(C, c, PO))
-                tt(out, c_(a, c), c_(C, c, PO), minus)
+            vv("eb", eb, E, b, mul)
             if pe3:
+                vv("ta", "q1", eb, C, mul)
                 for P, x in ((R[3], "bt"), (R[0], "q1")):
                     for c in two:
-                        mms([(c_(P, c, PO), S("idf"), c_(x, c), False, True)])
+                        mms([(c_(P, c, PO), S("nif"), c_(x, c), False, True)])
+            elif last and "a" in opt["fd"]:
+                vv("ta", ("tw", base), eb, C, mul)
+                adds("fa", ("tw", base), a)
+            else:
+                Y = X if last else C
+                vv("ta", Y, eb, C, mul)
+                vv("an", ("tw", base) if t < 2 else "q1", a, Y, plus)
             if last:
-                for c in two:
-                    if opt["pe_m"]:
-                        mm(c_(E, c, PO), S("jw"), c_(ab, c), S("nib"), c_(yw, c))
-                    else:
-                        tt(c_(E, c, PO), c_(ab, c), c_(E, c, PO), plus)
-                for c in two:
-                    tt(c_(ab, c), c_(yw, c, K), c_(E, c, PO), mul)
+                pe(E, ("jw", ab, 0), ("idb", yw, 0))
+                vv("cm", ab, (yw, K), E, mul)
+                for sq, x in zip(cof[t], (a, b)):
+                    square(sq, x)
+                    vv("cf", sq, sq, C, mul)
+                    if t == 2:
+                        act(S(sq, 0, K), S(sq, 0, K), Ident, 1.0, 1.0)
             elif t > 0:
-                if opt["m_dma"]:
+                if str(t) in opt["m_dma"]:
                     for c in two:
                         act(c_("xs", c), c_(E, c, PO))
-                    gdma(S(ab), S("xs"))
+                    adds("m", ab, "xs")
                 else:
-                    for c in two:
-                        tt(c_(ab, c), c_(ab, c), c_(E, c, PO), plus)
-        for P, v, new, on in ((R[3], vb, "bt", "b"), (R[2], "vaa", "q1", "a")) if not pe3 else ():
-            for c in two:
-                if on in opt["pe_init"]:
-                    mm(c_(P, c, PO), S("nif"), c_(new, c), S("idb"), c_(v, c))
-                else:
-                    tt(c_(P, c, PO), c_(v, c), c_(P, c, PO), minus)
+                    vv("m", ab, ab, E, plus)
         for t in range(TV - 1, -1, -1):
             a, b, yw, ab, ea, eb = "a%d" % t, bn[t], "yw%d" % t, "ab%d" % t, "ea%d" % t, "eb%d" % t
-            if t == 0 and not last:
-                win = S("dw", 0, O2)
-                for i, c in enumerate(three):
-                    act(c_("da", c), I(win, o_(ga[0], c)), scale=-1.0)
-                    if i > 0:
-                        act(c_("db", two[i - 1]), I(win, o_(gb[0], two[i - 1])), scale=-1.0)
-                for i, c in enumerate(three):
-                    tt(c_(R[0], c, PO), c_(R[0], c, PO), c_("da", c), mul)
-                    if i > 0:
-                        tt(c_("xs", two[i - 1]), c_(R[3], two[i - 1], PO), c_("db", two[i - 1]), mul)
-                for c in two:
-                    tt(c_("xs", c), c_(R[0], c, PO), c_("xs", c), plus)
-                for c in two:
-                    tt(c_(R[2], c, PO), c_(R[2], c, PO), c_(ls, c), plus)
-                for c in two:
-                    tt(c_("up", c), c_(R[2], c, PO), c_("xs", c), AluOpType.is_gt)
-                break
-            DA, DB, Q, Q2 = [(R[3], R[2], R[0], R[1]), (R[1], R[0], R[2], R[3]), (R[2], R[3], R[0], R[1])][t]
-            if pe3:
-                DA, DB, Q, Q2 = [(R[3], R[0], R[1], R[2]), (R[1], R[2], R[0], R[3]), (R[0], R[3], R[2], R[1])][t]
-            aa, bb = "aa%d" % (t % 2), "bb%d" % (t % 2)
-            if not last:
-                act(S(aa), S(a), Square)
-                act(S(bb), S(b), Square)
-            elif t != 1:
-                coef(aa, a, Q, yw)
-                coef(bb, b, Q2, yw)
-            if t < 2:
-                win = S("dw", 0, O1 if t == 1 else O2)
-                for c in two:
-                    for d, D, lst in (("da", DA, ga[t]), ("db", DB, gb[t])):
-                        act(c_(d, c), I(win, o_(lst, c)))
-                        if d in opt["pe_cp"]:
-                            mm(c_(D, c, PO), S("idf"), c_(d, c))
-                        else:
-                            act(c_(D, c, PO), c_(d, c))
             base = O0 + 2 * K * (2 - t)
+            outb, outa = ("dw", base + K) if k == 0 else "bt", ("dw", base)
+            win = S("dw", 0, O1 if t == 1 else O2)
+            if t == 2 and not last:
+                DA, DB, Wt, Q = R[2], R[3], R[0], R[1]
+                pe(DB, ("nif", "bt", 0), ("idb", vb, 0))
+                pe(DA, ("nif", "q1", 0), ("idb", "vaa", 0))
+                square("aa0", a)
+                square("bb0", b)
+                if opt["mid2"]:
+                    pe(Wt, ("idb", yw, K))
 
-            def terms():
-                if t == 2:
-                    for c in wide:
-                        tt(c_("pa", c), c_(eb, c), c_(DA, c, PO), mul)
-                        tt(c_("pb", c), c_(ea, c), c_(DB, c, PO), mul)
-                    send([([S("pa"), S("pb")], -2 * STEP, S(lu))], relay=True)
-                    return
-                u = "u1" if t == 1 else "lu1"
-                for c in two:
-                    if opt["fuse"]:
-                        tt(c_(u, c), I(win, o_(gb[t], c)), c_(ea, c), mul)
+                def first(n, sq, D1, D2, t2, P):
+                    vv("p" + n, sq, sq, D1, mul)
+                    if n in opt["mid2"]:
+                        vv("p" + n, t2, ab, D2, mul)
+                        adds("s" + n, sq, t2)
                     else:
-                        tt(c_(u, c), c_(ea, c), c_(DB, c, PO), mul)
-                if t == 1:
-                    for c in two:
-                        tt(c_("q1", c), c_(eb, c), c_(DA, c, PO), mul)
-                    send([([S("u1"), S("q1")], -STEP, S(ls))], relay=True)
-                    return
-                for c in two:
-                    tt(c_(Q2, c, PO), c_(eb, c), c_(DA, c, PO), mul)
-                    tt(c_("da", c), c_(Q2, c, PO), c_(u, c), plus)
-                gdma(S(lu), S(ls))
-                gdma(S("da", 0, K), S(lu))
-                act(S("pa"), I(S("da", 0, K), S("pos")), scale=0.125)
-                dma(lambda T: T.yh[:], lambda T: T.pa[:], [S("pa")], [], 500e3)
+                        vv("p" + n, P, ab, D2, mul)
 
-            def side(sq, D1, D2, P, t1, out, base, cs):
-                for c in cs:
-                    tt(c_(t1, c), c_(sq, c), c_(D1, c, PO), mul)
-                    tt(c_(P, c, PO), c_(ab, c), c_(D2, c, PO), mul)
-                if last:
-                    for c in cs:
-                        tt(c_(out, c, base), c_(t1, c), c_(P, c, PO), minus)
-                    return
-                for c in wide:
-                    tt(c_(P, c, PO), c_(t1, c), c_(P, c, PO), plus)
-                for c in wide:
-                    tt(c_(t1, c), c_(yw, c, K), c_(P, c, PO), mul)
-                for c in wide:
-                    tt(c_(out, c, base), c_(D1, c, PO), c_(t1, c), minus)
+                def second(n, sq, D1, P, out):
+                    if n in opt["mid2"]:
+                        vv("w", sq, sq, Wt, mul)
+                    else:
+                        vv("w", P, sq, P, plus)
+                        vv("w", sq, (yw, K), P, mul)
+                    vv("w", out, D1, sq, minus)
 
-            if t < 2:
-                terms()
-            side(aa, DB, DA, Q, "xs", *(("dw", base + K) if k == 0 else ("bt", 0)), two)
-            back("dw", base + K, t)
-            side(bb, DA, DB, Q2, "da" if t == 1 else "q1" if t == 2 else "ls1", "dw", base, wide)
-            if t == 2:
-                if last:
-                    coef("aa1", "a1", Q, "yw1")
-                    coef("bb1", "b1", Q2, "yw1")
-                terms()
-            if t == 1 and not last:
-                for P, x in ((R[0], "eb0"), (R[3], "ea0"), (R[2], lu)):
-                    for c in two:
-                        mm(c_(P, c, PO), S("idf"), c_(x, c))
+                def terms():
+                    vv("t2", "pa", eb, DA, mul)
+                    vv("t2", "pb", ea, DB, mul)
+                    send([([S("pa"), S("pb")], -2 * STEP, S(lu))], own=opt["own"]["t2"])
+                Qa = Q if opt["mid2"] else Wt
+                steps = dict(b=lambda: first("b", "aa0", DB, DA, "xs", Q), a=lambda: first("a", "bb0", DA, DB, "q1", Qa), t=terms,
+                             B=lambda: (second("b", "aa0", DB, Q, outb), back("dw", base + K, t)),
+                             A=lambda: second("a", "bb0", DA, Qa, outa))
+                for x in opt["ord2"]:
+                    steps[x]()
+            elif t == 1 and not last:
+                AA, M, BB, Wt = R[1], R[3], R[0], R[2]
+                square(AA, a)
+                pe(M, ("idf", ab, 0))
+                square(BB, b)
+                if opt["mid1"]:
+                    pe(Wt, ("idb", yw, K))
+                picks("db", "db", win, gb[t], two)
+                picks("da", "da", win, ga[t], two)
+
+                def first(n, P, d1, d2, t1, t2):
+                    if n in opt["mid1"]:
+                        vv("p" + n, t1, d1, P, mul)
+                        vv("p" + n, t2, d2, M, mul)
+                        adds("s" + n, t1, t2)
+                    else:
+                        vv("p" + n, P, d1, P, mul)
+                        vv("p" + n, t2, d2, M, mul)
+
+                def second(n, P, d1, t1, t2, out):
+                    if n in opt["mid1"]:
+                        vv("w", P, t1, Wt, mul)
+                    else:
+                        vv("w", P, t2, P, plus)
+                        vv("w", P, (yw, K), P, mul)
+                    vv("w", out, d1, P, minus)
+                steps = dict(b=lambda: first("b", AA, "db", "da", "aa1", "xs"), a=lambda: first("a", BB, "da", "db", "bb1", "aa0"),
+                             u=lambda: vv("u", "u1", (win, gb[t]), ea, mul), q=lambda: vv("u", "q1", (win, ga[t]), eb, mul),
+                             t=lambda: send([([S("u1"), S("q1")], -STEP, S(ls))], own=opt["own"]["t1"]),
+                             B=lambda: (second("b", AA, "db", "aa1", "xs", outb), back("dw", base + K, t)),
+                             A=lambda: second("a", BB, "da", "bb1", "aa0", outa))
+                for x in opt["ord1"]:
+                    steps[x]()
+            elif not last:
+                P, L, Z = R[3], R[1], R[2]
+                pe(P, ("idf", eb, 0))
+                pe(L, ("nif", lu, 0))
                 for c in two:
-                    mms([(c_(R[1], c, PO), S("bm"), S("one"), True, False)])
+                    mms([(c_(Z, c, PO), S("bm"), S("one"), True, False)])
+                picks("", "da", win, ga[t], two)
+                vv("u", "xs", (win, gb[t]), ea, mul)
+                vv("h", P, P, "da", mul)
+                vv("h", "xs", P, "xs", plus)
+                vv("h", L, L, ls, minus)
+                vv("up", "up", "xs", L, AluOpType.is_gt)
+            elif t == 2:
+                DA, DB, Q = R[0], R[3], R[1]
+
+                def side(n, sq, D1, D2, t2, out):
+                    if n in opt["fin"][t]:
+                        vv("p3", out, sq, D1, mul)
+                        vv("p3", t2, ab, D2, mul)
+                        adds("z" + n, out, t2)
+                    else:
+                        vv("p3", sq, sq, D1, mul)
+                        vv("p3", Q, ab, D2, mul)
+                        vv("p3", out, sq, Q, plus)
+
+                def terms():
+                    vv("t2", "pa", eb, DA, mul)
+                    vv("t2", "pb", ea, DB, mul)
+                    send([([S("pa"), S("pb")], -2 * STEP, S(lu))], own=opt["own"]["t2"])
+                steps = dict(b=lambda: (side("b", cof[t][0], DB, DA, "xs", outb), back("dw", base + K, t)),
+                             a=lambda: side("a", cof[t][1], DA, DB, "q1", outa), t=terms)
+                for x in opt["ord3"][t]:
+                    steps[x]()
+            else:
+                CB, CA, CM = (R[2], R[1], R[3]) if t == 1 else (R[0], R[2], R[3])
+                pe(CB, ("idf", cof[t][0], 0), ("idb", "one", 0))
+                pe(CA, ("idf", cof[t][1], 0), ("idb", "one", 0))
+                pe(CM, ("idf", ab, 0))
+                picks("db", "db", win, gb[t], two)
+                picks("da", "da", win, ga[t], two)
+                u, q = ("u1", "q1") if t == 1 else ("lu1", "ls1")
+
+                def side(n, P, d1, d2, t2, out):
+                    if n in opt["fin"][t]:
+                        vv("p3", out, d1, P, mul)
+                        vv("p3", t2, d2, CM, mul)
+                        adds("z" + n, out, t2)
+                    else:
+                        vv("p3", P, d1, P, mul)
+                        vv("p3", t2, d2, CM, mul)
+                        vv("p3", out, t2, P, plus)
+
+                def terms():
+                    if t == 1:
+                        send([([S(u), S(q)], -STEP, S(ls))], own=opt["own"]["t1"])
+                        return
+                    gdma(S(lu), S(u))
+                    for c in two:
+                        mms([(c_(R[1], c, PO), S("idb"), S("one"), True, False), (c_(R[1], c, PO), S("nib"), S("one"), False, False)])
+                    for x in (q, lu, ls):
+                        for c in range(2):
+                            mms([(S(R[1], PO + s * KW, PO + (s + 1) * KW), S("idf"), (x, s, K, 16), False, x == ls and s % 8 == 7)
+                                 for s in range(8 * c, 8 * c + 8)])
+                    for c in two:
+                        act(c_("pa", c), c_(R[1], c, PO), scale=0.125)
+                    dma(lambda T: T.yh[:], lambda T: T.pa[:], [S("pa")], [], 500e3)
+                steps = dict(b=lambda: (side("b", CB, "db", "da", "xs", outb), back("dw", base + K, t)),
+                             a=lambda: side("a", CA, "da", "db", "a2", outa), t=terms,
+                             u=lambda: vv("u", u, (win, gb[t]), ea, mul), q=lambda: vv("u", q, (win, ga[t]), eb, mul))
+                for x in opt["ord3"][t]:
+                    steps[x]()
         if last:
-            for c in range(2):
-                out, src = S("wf", c * W // 2, (c + 1) * W // 2), I(S("dw", 0, O2 + 2 * K), S("hl", c * 64, (c + 1) * 64))
-                if c == 0:
+            n = opt["outs"]
+            for c in range(len(n)):
+                lo, hi = c * W // len(n), (c + 1) * W // len(n)
+                out, src = S("wf", lo, hi), I(S("dw", 0, O2 + 2 * K), S("hl", lo // 16, hi // 16))
+                if n[c] == "v":
                     ts(out, src, -1.0, mul)
                 else:
                     act(out, src, scale=-1.0)
-                dma(lambda T, c=c: T.yd[:, c * W // 2:(c + 1) * W // 2], lambda T, c=c: T.wf[:, c * W // 2:(c + 1) * W // 2],
-                    [out], [], 520e3)
+                dma(lambda T, lo=lo, hi=hi: T.yd[:, lo:hi], lambda T, lo=lo, hi=hi: T.wf[:, lo:hi], [out], [], 1050e3 / len(n),
+                    q="y" if n[c] == "v" else "s")
             break
-        Z = R[1]; n = k + 1; lw = "lw%d" % n
+        n = k + 1; lw = "lw%d" % n
+        fill(S("da", 0, 1), LOW)
         mms([(S(Z, PO + s * KW, PO + (s + 1) * KW), S("vm"), ("up", s, K, 16), False, s % 8 == 7) for s in range(16)])
-        scan(S("db"), S(Z, PO, PO + K), S("kr"), -1.0)
-        ts(S("da", 0, 1), S("db", K - 1), -JM * 1024, plus)
-        scan(S("da", 1, K + 1), S(Z, PO, PO + K), S("kr"), S("da", 0, 1))
+        scan(S("da", 1, K + 1), S(Z, PO, PO + K), S("kr"), LOW)
+        ts(S("end"), S("hot"), S("da", K, K + 1), mul, LOW / 16, plus)
+        mms([(S(Z, 0, 16), S("onf"), S("end"), True, True)])
         for lists, grp in (([5], "p%d" % n), ([0], "i%d" % n), ([1, 2, 3, 4], "o%d" % n)):
             for i in lists:
                 wrap(S("wp", i * KW, (i + 1) * KW), S("da", 0, K), rows[i], grp)
-                wrap(S("wc", i * KW, (i + 1) * KW), S("da", 1, K + 1), rows[i], grp)
+                wrap(S("wc", i * KW, (i + 1) * KW), S("da", 1, K + 1), rows[i], grp, "s" if i == 5 else "y")
             lo, hi = lists[0] * KW, (lists[-1] + 1) * KW
             tt(S("wp", lo, hi), S("wp", lo, hi), S("wc", lo, hi), minus)
-            tt(S("br", lo, hi), S("wp", lo, hi), S("kw", lo, hi), plus)
+            tt(S("wp", lo, hi), S("wp", lo, hi), S("kw", lo, hi), plus)
+            for i in lists:
+                ts(S("br", i * KW, (i + 1) * KW), S("wp", i * KW, (i + 1) * KW), S(Z, rows[i], rows[i] + 1), mx)
             ts(S("br", 400 + lo, 400 + hi), S("br", lo, hi), int(JM) - 1, AluOpType.bitwise_and)
             cp(S(lw, lo, hi), S("br", 400 + lo, 400 + hi))
         send([([S(lw, 2 * KW, 4 * KW)], STEP, S("v1%d" % n)), ([S(lw, 4 * KW)], 2 * STEP, S("v2%d" % n))], also=[S(lu), S(ls)])
@@ -660,14 +722,15 @@ def build(opt):
 
 def times(ops, m):
     cost = [o["cost"](m) for o in ops]
-    lat = [o["lat"](m) if o["lat"] else 0.0 for o in ops]
+    ways = [o["lat"](m) if o["lat"] else [] for o in ops]
+    lat = [max([a + b + max(c, 0.0) for a, r, b, c in w] + [0.0]) for w in ways]
     gap = [0.0 if o["kind"] == "r" else m["hop"] for o in ops]
-    return cost, lat, gap
+    return cost, lat, gap, ways
 
 
 def replay(ops, seq, tm):
-    cost, lat, gap = tm
-    free, st, fin = {}, [0.0] * len(ops), [0.0] * len(ops)
+    cost, lat, gap, ways = tm
+    free, st, fin, arr = {}, [0.0] * len(ops), [0.0] * len(ops), {}
     for i in seq:
         o = ops[i]; s = free.get(o["q"], 0.0)
         for d in o["deps"]:
@@ -675,50 +738,97 @@ def replay(ops, seq, tm):
                 s = fin[d] + gap[i]
         if o["q"] != "-":
             free[o["q"]] = s + cost[i]
-        st[i] = s; fin[i] = s + cost[i] + lat[i]
+        elif arr.get(o["deps"][0], 0.0) > s:
+            s = arr[o["deps"][0]]
+        st[i] = s; s += cost[i]; f = s
+        for a, r, b, c in ways[i]:
+            e = max(s + a, free.get(r, 0.0)) + b
+            if r:
+                free[r] = e
+            if c < 0:
+                arr[i] = e
+            elif e + c > f:
+                f = e + c
+        fin[i] = f
     return st, fin
 
 
-def place(ops, key, tm):
-    cost, lat, gap = tm
-    n = len(ops); busy, st, fin = {}, [0.0] * n, [0.0] * n
-    turn = sorted(range(n), key=lambda i: (key[i], i))
+def place(qs, links, turn, pre, cost, post):
+    n = len(qs); busy, st, fin = {}, [0.0] * n, [0.0] * n
     for i in turn:
-        o = ops[i]; s = 0.0
-        for d in o["deps"]:
-            if fin[d] + gap[i] > s:
-                s = fin[d] + gap[i]
-        if o["q"] != "-":
-            line = busy.setdefault(o["q"], []); p = len(line)
+        s = 0.0
+        for d in links[i]:
+            if fin[d] > s:
+                s = fin[d]
+        s += pre[i]; c = cost[i]
+        if qs[i] != "-":
+            line = busy.setdefault(qs[i], []); p = len(line)
             while p > 0 and line[p - 1][1] > s:
                 p -= 1
-            while p < len(line) and line[p][0] < s + cost[i]:
-                s = max(s, line[p][1]); p += 1
-            line.insert(p, (s, s + cost[i]))
-        st[i] = s; fin[i] = s + cost[i] + lat[i]
-    return sorted(turn, key=lambda i: st[i])
+            while p < len(line) and line[p][0] < s + c:
+                if line[p][1] > s:
+                    s = line[p][1]
+                p += 1
+            line.insert(p, (s, s + c))
+        st[i] = s; fin[i] = s + c + post[i]
+    return st
 
 
 def order(ops, tries, seed=1):
     tms = [times(ops, m) for m in SPREAD]; rng = np.random.default_rng(seed); n = len(ops)
-    best = None; own = [float(i) if o["main"] else float(n + i) for i, o in enumerate(ops)]
-    for it in range(tries):
-        new = list(own if best is None else best[2])
-        if best is not None:
-            for j in rng.integers(0, n, 1 + it % 3):
-                new[j] = best[3][j] + float(rng.normal()) * (3.0, 10.0, 40.0)[it % 3]
-        key = list(new)
+    qs = [o["q"] for o in ops]; before = [o["deps"] for o in ops]; after = [[] for o in ops]
+    for i, o in enumerate(ops):
+        for d in o["deps"]:
+            after[d].append(i)
+
+    def forth(key, tm):
+        key = list(key)
         for i in range(n - 1, -1, -1):
-            for d in ops[i]["deps"]:
+            for d in before[i]:
                 if key[i] < key[d]:
                     key[d] = key[i]
-        seq = place(ops, key, tms[0])
-        first = max(replay(ops, seq, tms[0])[1])
-        if best is not None and first > best[4] + 1.5:
-            continue
-        val = first + sum(max(replay(ops, seq, tm)[1]) for tm in tms[1:])
-        if best is None or val <= best[0]:
-            best = (val, seq, new, key, first)
+        st = place(qs, before, sorted(range(n), key=lambda i: (key[i], i)), tm[2], tm[0], tm[1])
+        return sorted(range(n), key=lambda i: (st[i], i))
+
+    def late(seq, tm):
+        st, fin = replay(ops, seq, tm)
+        st = place(qs, after, sorted(range(n), key=lambda i: (-fin[i], -i)), [fin[i] - st[i] - tm[0][i] for i in range(n)], tm[0], tm[2])
+        return [-(st[i] + tm[0][i]) for i in range(n)]
+
+    def value(seq, bar=1e9):
+        total = 0.0
+        for j, tm in enumerate(tms):
+            total += max(replay(ops, seq, tm)[1])
+            if j == 0 and total > bar:
+                return 1e9, 1e9
+            first = total if j == 0 else first
+        return total, first
+
+    best = None
+    for pace in (1.0, 1.2, 1.45, 2.0):
+        cost, lat, gap, ways = tms[0]; now = 0.0; key = [1e9] * n
+        for i, o in enumerate(ops):
+            if o["main"]:
+                key[i] = now; now += pace * cost[i]
+        for i in range(n - 1, -1, -1):
+            key[i] = min(key[i], now)
+            for d in before[i]:
+                key[d] = min(key[d], key[i] - pace * cost[d] - lat[d] - gap[i])
+        for rep in range(6):
+            seq = forth(key, tms[0]); val = value(seq)
+            if best is None or val[0] < best[0][0]:
+                best = (val, seq, key)
+            key = late(seq, tms[0])
+    for it in range(tries):
+        if it % 100 == 0:
+            key = late(best[1], tms[0])
+        else:
+            key = list(best[2])
+            for j in rng.integers(0, n, 1 + it % 3):
+                key[j] += float(rng.normal()) * (0.5, 2.0, 8.0)[it % 3]
+        seq = forth(key, tms[0]); val = value(seq, best[0][1] + 1.5)
+        if val[0] <= best[0][0]:
+            best = (val, seq, key)
     return best[1]
 
 
@@ -732,11 +842,11 @@ def rank_program(g, core, T, topo):
         served = [r for r, c in enumerate(T.cores) if topo.chip(c) == topo.chip(core) and helper(T, topo, c) == core]
         sent = 0
         for i, step, hold, land in sorted(RELAYS, key=lambda x: SEQ.index(x[0])) if served else []:
-            dst = T.cores[(served[0] + step) % N]; rid, pid, _ = topo.addr(dst); n = OPS[i]["cnt"] // 2
-            g.wait_ge(T.sem["h%d" % i], n)
+            dst = T.cores[(served[0] + step) % N]; rid, pid, _ = topo.addr(dst)
+            g.wait_ge(T.sem["h%d" % i], 8)
             g.remote_dma(ap(T, land), ap(T, hold), T.sem["a%d_%d" % (i, step % N)], T.sem.hand, pid, rid,
-                         sum(1 << e for e in topo.engines(core, dst)[:n]))
-            sent += n
+                         sum(1 << e for e in topo.engines(core, dst)[:8]))
+            sent += 8
         if sent:
             g.wait_ge(T.sem.hand, sent)
         return

import numpy as np
from concourse.bass import DstId, RemoteDMATransfer
from concourse.mybir import AluOpType, ActivationFunctionType

N, W, K, TV, STEP, RO = 8, 2048, 960, 3, 3, 3
H = K // 2
KW = K // 16
O0, O1, O2 = W, W + 2 * K, W + 4 * K
JM = 8192.0
LOW = -1024 * JM
PO = 32
OPT = dict(m_dma="12", put="sssvss", get="svvssvsvsssss", head=160, pa0="", fd="", mid2="ab", mid1="",
           ord2="batBA", ord1="uqtbBaA", ord3=["uqtba", "uqtba", "tba"], fin=["", "", ""], outs="vs",
           wide="w t2 cm cf".split(), half=[], own=dict(y=1, t2=1, t1=2))
TRIES = 12000
F32, BF, I32, U16 = "float32", "bfloat16", "int32", "uint16"

SCRATCH = {}
for _n, _c, _d in [
        ("tw", O2, F32), ("dw", O2 + W, F32), ("wf", W, F32), ("vj", K, F32), ("thb", W, BF), ("vab", W, BF),
        ("raw", 2 * K, BF), ("yw0", 2 * K, BF), ("yw1", 2 * K, BF), ("yw2", 2 * K, BF),
        ("a0", K, BF), ("b0s", K, BF), ("b0", K, BF), ("a1", K, F32), ("b1", K, F32), ("a2", K, F32), ("b2", K, F32),
        ("ab0", K, F32), ("ab1", K, F32), ("ab2", K, F32), ("ea0", K, F32), ("ea1", K, F32), ("ea2", K, F32),
        ("eb0", K, F32), ("eb1", K, F32), ("eb2", K, F32), ("aa0", K, F32), ("bb0", K, F32), ("aa1", K, F32),
        ("bb1", K, F32), ("bt", K, F32), ("q1", K, F32), ("xs", K, F32), ("pa", K, F32),
        ("pb", K, F32), ("u1", K, F32), ("da", K + 8, F32), ("db", K, F32),
        ("lu0", K, F32), ("ls0", K, F32), ("lu1", K, F32), ("ls1", K, F32),
        ("vaa", K, BF), ("vbs", K, BF), ("vbb", K, BF), ("kr", K, F32), ("br", K, I32), ("up", K, BF),
        ("ani", 3 * KW, I32), ("bri", KW, I32), ("n0", 2 * KW, U16), ("nb0", KW, U16), ("s1", 2 * KW, U16),
        ("s2", 2 * KW, U16), ("r1", 2 * KW, U16), ("r2", 2 * KW, U16),
        ("ia", 128, I32), ("fa", 128, F32), ("hot", 16, F32), ("end", 16, F32),
        ("pi", 8, I32), ("pj", 8, I32), ("pf", 8, F32), ("cw", 128, F32), ("jw", 128, F32), ("j6", 6 * KW, F32),
        ("rho", KW, U16), ("pos", KW, U16), ("rh2", 128, U16), ("po2", 128, U16),
        ("dl", 128, U16), ("hl", 128, U16), ("gw", 2 * KW, F32),
        ("f1", 2 * KW, U16), ("f2", 2 * KW, U16), ("g1", 2 * KW, U16), ("g0", 2 * KW, U16), ("home", 3 * KW, U16),
        ("kw", 6 * KW, F32), ("wp", 384, F32), ("wc", 384, F32), ("iw", KW, F32),
        ("lw1", 6 * KW, U16), ("lw2", 6 * KW, U16), ("v11", 2 * KW, U16), ("v12", 2 * KW, U16),
        ("v21", 2 * KW, U16), ("v22", 2 * KW, U16), ("x01", KW, U16), ("x02", KW, U16), ("x11", KW, U16),
        ("x12", KW, U16), ("x21", KW, U16), ("x22", KW, U16),
        ("one", H, BF), ("onf", 128, F32), ("idf", 128, F32), ("idb", 128, BF), ("nif", 128, F32), ("nib", 128, BF),
        ("vm", 128, BF), ("bm", 128, BF)]:
    SCRATCH[_n] = ("sbuf", [128, _c], _d)
for _i in range(4):
    SCRATCH["ps%d" % _i] = ("psum", [128, 1024], F32)
SIZE = {F32: 4, BF: 2, I32: 4, U16: 2}

NOM = dict(cyc=0.00102, gat=1.5, sca=3.5, fix=0.06, hop=0.12, pe=0.0005, dma=2.1, gdma=1.0, rem=1.2, net=2.5, bw=70e3,
           acc=300e3, blk=0.3)
SPREAD = [NOM, dict(NOM, gat=1.1, sca=2.0, cyc=0.0009), dict(NOM, gat=2.0, sca=5.5),
          dict(NOM, dma=3.0, net=4.0, bw=45e3, pe=0.0007, acc=200e3, blk=0.6)]


def S(name, lo=0, hi=None):
    return (name, lo, SCRATCH[name][1][1] if hi is None else hi)


def I(win, off):
    return ("#", win, off)


def ap(T, x):
    if x[0] == "#":
        return ap(T, x[1]).indirect(ap(T, x[2]))
    if len(x) == 4:
        return T[x[0]][:, x[1]:x[2]:x[3]]
    return T[x[0]][:, x[1]:x[2]]


def width(x):
    if x[0] == "#":
        return 16 * (x[2][2] - x[2][1])
    return (x[2] - x[1] + x[3] - 1) // x[3] if len(x) == 4 else x[2] - x[1]


def psum(x):
    return x[0] != "#" and x[0].startswith("ps")


def transfer(topo, dst, mask, sem, srcs, land):
    rid, pid, _ = topo.addr(dst)
    return RemoteDMATransfer(dst_ids=[DstId(rid=rid, pnc=pid)], dma_engine_mask=mask, remote_sem=sem, srcs=srcs, dsts=[land],
                             alu_op=1 if len(srcs) > 1 else 0)


def helper(T, topo, core):
    mine = [c for c in T.cores if topo.chip(c) == topo.chip(core)]
    free = [c for c in topo.cores_of(core) if topo.die(c) != topo.die(core) and c not in T.cores
            and all(topo.may_write(c, d) for d in T.cores)]
    return free[mine.index(core)]


def build(opt):
    ops, relays = [], []
    sems = ["cv", "cs", "ct", "cg", "hand"]
    wr, rd, main = {}, {}, [False]

    def span(x):
        sz = SIZE[SCRATCH[x[0]][2]]
        b = 2048 if psum(x) else 16
        return x[0], x[1] * sz // b * b, -(-x[2] * sz // b) * b

    def add(q, fn, reads, writes, cost, kind="c", lat=None, group=None, after=(), cnt=16):
        i = len(ops); deps = set(after)
        rs, ws = [], []
        for x in reads:
            rs += [x[1], x[2]] if x[0] == "#" else [x]
        for x in writes:
            if x[0] == "#":
                ws.append(x[1]); rs.append(x[2])
            else:
                ws.append(x)
        for x in rs:
            n, lo, hi = span(x)
            deps.update(j for a, b, j in wr.get(n, []) if a < hi and lo < b)
            if psum(x):
                deps.update(j for a, b, j in rd.get(n, []) if a < hi and lo < b and ops[j]["q"] != q)
        for x in ws:
            n, lo, hi = span(x)
            if kind != "r":
                deps.update(j for a, b, j in wr.get(n, []) + rd.get(n, []) if a < hi and lo < b)
        for x in rs:
            n, lo, hi = span(x)
            rd.setdefault(n, []).append((lo, hi, i))
        for x in ws:
            n, lo, hi = span(x)
            wr[n] = [e for e in wr.get(n, []) if not (lo <= e[0] and e[1] <= hi)] + [(lo, hi, i)]
            rd[n] = [e for e in rd.get(n, []) if e[2] == i or not (lo <= e[0] and e[1] <= hi)]
        deps.discard(i)
        if group is not None:
            for j in [j for j in deps if ops[j]["group"] == group]:
                deps.discard(j); deps.update(ops[j]["deps"])
        if kind != "c" and group is None:
            group = "d%d" % i
        if group is not None and group not in sems:
            sems.append(group)
        ops.append(dict(q=q, fn=fn, deps=deps, cost=cost, kind=kind, lat=lat, group=group, cnt=cnt, main=main[0] and q == "v",
                        nm=[x[:3] if x[0] != "#" else x[1] for x in writes][:1]))
        return i

    def ecost(out, ins, two):
        n = width(out)
        if out[0] == "#":
            return lambda m: m["fix"] + n * m["sca"] * m["cyc"]
        if ins and ins[0][0] == "#":
            return lambda m: m["fix"] + n * m["gat"] * m["cyc"]
        return lambda m: m["fix"] + max(64, n * two) * m["cyc"]

    def tt(out, x, y, op):
        two = 1 if psum(x) or psum(y) else 2
        return add("v", lambda g, T, c: g.vector.tensor_tensor(ap(T, out), ap(T, x), ap(T, y), op), [x, y], [out], ecost(out, [x], two))

    def ts(out, x, s1, op0, s2=None, op1=None):
        col = [s for s in (s1, s2) if isinstance(s, tuple)]

        def fn(g, T, c):
            a = ap(T, s1) if isinstance(s1, tuple) else s1
            if op1 is None:
                return g.vector.tensor_scalar(ap(T, out), ap(T, x), a, None, op0)
            return g.vector.tensor_scalar(ap(T, out), ap(T, x), a, ap(T, s2) if isinstance(s2, tuple) else s2, op0, op1)
        return add("v", fn, [x] + col, [out], ecost(out, [x], 1))

    def cp(out, x):
        return add("v", lambda g, T, c: g.vector.tensor_copy(ap(T, out), ap(T, x)), [x], [out], ecost(out, [x], 1))

    def fill(out, v):
        return add("v", lambda g, T, c: g.vector.memset(ap(T, out), v), [], [out], ecost(out, [], 1))

    def scan(out, d0, d1, init):
        return add("v", lambda g, T, c: g.vector.tensor_tensor_scan(ap(T, out), ap(T, d0), ap(T, d1), init, AluOpType.max, AluOpType.min),
                   [d0, d1], [out], ecost(out, [d0], 1))

    def act(out, x, func=ActivationFunctionType.Copy, scale=None, bias=None):
        def fn(g, T, c):
            if bias is not None:
                return g.scalar.activation(ap(T, out), ap(T, x), func, bias=bias, scale=scale)
            if scale is None:
                return g.scalar.activation(ap(T, out), ap(T, x), func)
            return g.scalar.activation(ap(T, out), ap(T, x), func, scale=scale)
        return add("s", fn, [x], [out], ecost(out, [x], 1))

    def mms(parts):
        n = sum(max(64, width(p[2])) * (4 if SCRATCH[p[2][0]][2] == F32 else 1) for p in parts)

        def fn(g, T, c):
            for out, lhs, rhs, start, stop in parts:
                ins = g.tensor.matmul(ap(T, out), ap(T, lhs), ap(T, rhs), start, stop)
            return ins
        return add("t", fn, [x for p in parts for x in p[1:3]], [p[0] for p in parts], lambda m: 0.03 * len(parts) + n * m["pe"])

    def iota(out, pat, base, cm):
        fl = SCRATCH[out[0]][2] != I32

        def fn(g, T, c):
            if fl:
                return g.iota(ap(T, out), pat, base, cm, allow_small_or_imprecise_dtypes=True)
            return g.iota(ap(T, out), pat, base, cm)
        return add("g", fn, [], [out], lambda m: 0.13 + 2 * width(out) * m["cyc"])

    def keep(out, x, pat, op, base, cm):
        return add("g", lambda g, T, c: g.affine_select(ap(T, out), ap(T, x), pat, op, 0.0, base, cm), [x], [out], lambda m: 0.43)

    def dma(fo, fi, reads, writes, nb, group=None, q="y"):
        def fn(g, T, c):
            return (g.sync if q == "y" else g.scalar).dma_start(fo(T), fi(T))
        big = nb > 250e3
        return add(q, fn, reads, writes, lambda m: 0.1, "d",
                   lambda m: [(m["dma"] - 1.0, "E", nb / 600e3 if big else 0.05, 1.0 if big else 1.0 + nb / 600e3)], group)

    def gdma(out, src, acc=True):
        def fn(g, T, c):
            if acc:
                return g.dma_start(ap(T, out), ap(T, src), accum_op=AluOpType.add)
            return g.dma_start(ap(T, out), ap(T, src))
        return add("g", fn, [src, out] if acc else [src], [out], lambda m: m["gdma"], "d",
                   lambda m: [(m["dma"] - 1.0, "E", width(out) * 512 / m["acc"], 1.0)])

    def wrap(out, src, row, group=None, q="y"):
        return dma(lambda T: ap(T, out), lambda T: T[src[0]][row::16, src[1]:src[2]], [src], [out], 200e3, group, q)

    def unwrap(out, row, src, group=None):
        return dma(lambda T: T[out[0]][row::16, out[1]:out[2]], lambda T: ap(T, src), [src], [out], 200e3, group)

    def send(parts, also=(), own=0):
        i = len(ops); hand = None
        if own:
            (srcs, step, land), = parts
            h = (land[2] - land[1]) // (own + 1)
            parts = [([S(x[0], x[1] + j * h, x[1] + (j + 1) * h) for x in srcs], step, S(land[0], land[1] + j * h, land[1] + (j + 1) * h))
                     for j in range(own + 1)]
            hand, _, upper = parts.pop()
            hold = upper if land[0].startswith("yw") else S("dw", len(relays) * H, len(relays) * H + h)
            relays.append((i, step, hold, upper)); sems.append("h%d" % i)
        per = 8 // (1 << (len(parts) - 1).bit_length())
        names = {}
        for srcs, step, land in parts:
            names.setdefault(step, []).append(land)

        def fn(g, T, c):
            tr = []; used = 0
            for k, (srcs, step, land) in enumerate(parts):
                dst = T.cores[(c["rank"] + step) % N]
                mask = sum(1 << e for e in c["topo"].engines(c["core"], dst)[k * per:(k + 1) * per]); used += mask
                tr.append(transfer(c["topo"], dst, mask, T.sem["a%d_%d" % (i, step % N)], [ap(T, s) for s in srcs], ap(T, land)))
            if hand:
                by = helper(T, c["topo"], c["core"])
                eng = [e for e in c["topo"].engines(c["core"], by) if not used >> e & 1][:8]
                tr.append(transfer(c["topo"], by, sum(1 << e for e in eng), T.sem["h%d" % i], [ap(T, s) for s in hand], ap(T, hold)))
            return g.remote_dma_fused(tr, local_sem=T.sem["d%d" % i])
        nb = sum(128 * width(p[0][0]) * SIZE[SCRATCH[p[0][0][0]][2]] for p in parts)
        add("g", fn, [s for p in parts for s in p[0]] + (hand or []), list(also), lambda m: m["rem"], "x",
            lambda m: [(1.0, "E", 0.3 + m["blk"] * 2 * nb / m["bw"], 0.0), (1.0, "L", 2 * nb / m["bw"], 0.0)]
            + ([(1.0 + nb / own / 100e3 + m["net"] + m["rem"], "M", 2 * nb / own / m["bw"], -1.0)] if hand else []),
            cnt=per * len(parts) + (8 if hand else 0))
        for step, lands in names.items():
            add("-", None, [], lands + ([upper] if hand else []), lambda m: 0.0, "r", lambda m: [(m["net"] - 1.0, "", 0.0, 0.0)],
                "a%d_%d" % (i, step % N), after=[i], cnt=per * len(lands) + (8 if hand else 0))

    mul, plus, minus, mx = AluOpType.mult, AluOpType.add, AluOpType.subtract, AluOpType.max
    Silu, Square, Ident = ActivationFunctionType.Silu, ActivationFunctionType.Square, ActivationFunctionType.Identity

    def tolist(out, src, sub=0):
        ts(out, src, 0.25 - sub, plus)

    def places(out, n):
        ts(S("ia", 0, n), S("cw", 0, n), -(n - 1) / 2.0, plus, 1.0 / n, mul)
        ts(S("fa", 0, n), S("ia", 0, n), -(16 * n - 1) / 16.0, mul)
        tt(S("fa", 0, n), S("fa", 0, n), S("cw", 0, n), plus)
        ts(out, S("fa", 0, n), 16.0, mul)

    fill(S("br"), 0)
    dma(lambda T: T.ani[:], lambda T: T.an[:], [], [S("ani")], 90e3, "names")
    dma(lambda T: T.bri[:], lambda T: T.bn[0::TV, :], [], [S("bri")], 200e3, "names")
    for t in range(TV):
        dma(lambda T, t=t: T.br[4 * t::16, :], lambda T, t=t: T.bn[t::TV, :], [], [S("br")], 100e3, "rows")
    dma(lambda T: T.raw[:, :K], lambda T: T.yt[:], [], [S("raw", 0, K)], 260e3, q="s")
    dma(lambda T: T.thb[:], lambda T: T.th[:], [], [S("thb")], 520e3, q="s")
    dma(lambda T: T.raw[:, K:], lambda T: T.wt[:], [], [S("raw", K)], 260e3, q="s")
    dma(lambda T: T.vab[:], lambda T: T.va[:], [], [S("vab")], 520e3)
    iota(S("pi", 0, 1), [[0, 1]], 0, 1)
    iota(S("cw"), [[16, 128]], 0, 0)
    iota(S("jw"), [[1, 128]], 0, 0)
    iota(S("wf", 0, 512), [[1, 512]], 0, 0)
    iota(S("dw", O0, O0 + K), [[1, 16], [16, KW]], O0, 0)
    iota(S("vj"), [[1, K]], O0 + K, 0)
    ts(S("pj", 0, 1), S("pi", 0, 1), 15, AluOpType.bitwise_and)
    cp(S("pf", 0, 1), S("pj", 0, 1))
    ts(S("cw"), S("cw"), S("pf", 0, 1), plus)
    ts(S("pf", 4, 5), S("pf", 0, 1), float(KW), mul)
    ts(S("rho"), S("jw", 0, KW), S("pf", 4, 5), plus)
    places(S("pos"), KW)
    act(S("wf", 512, 1024), S("wf", 0, 512), Ident, 1.0, 512.0)
    act(S("wf", 1024), S("wf", 0, 1024), Ident, 1.0, 1024.0)
    cp(S("n0", 0, KW), S("ani", 0, KW))
    cp(S("n0", KW), S("bri"))
    cp(S("s1", 0, KW), S("ani", KW, 2 * KW))
    cp(S("s2", 0, KW), S("ani", 2 * KW))
    cp(S("lu1"), I(S("br"), S("pos")))
    for t in range(TV):
        wrap(S("wp", t * KW, (t + 1) * KW), S("lu1"), 4 * t, "wrapb")
    cp(S("s1", KW), S("wp", KW, 2 * KW))
    cp(S("s2", KW), S("wp", 2 * KW, 3 * KW))
    cp(S("nb0"), S("wp", 0, KW))
    send([([S("s1")], STEP, S("r1")), ([S("s2")], 2 * STEP, S("r2"))])
    who = {k: list(opt[k]) for k in ("put", "get")}
    wa, wb = S("wf"), S("dw", O2)

    def put(table, lst, val):
        if who["put"].pop(0) == "v":
            cp(I(table, lst), val)
        else:
            act(I(table, lst), val, Silu)

    def get(out, src, f=1.0):
        if who["get"].pop(0) == "v":
            ts(out, src, f, mul)
        else:
            act(out, src, scale=f)

    put(wa, S("n0", 0, KW), S("dw", O0, O0 + K))
    put(wa, S("n0", KW), S("vj"))
    sw0, sw1, l2, l1, lh = S("wc", 0, 128), S("wc", 128, 256), S("wp", 0, 128), S("wp", 128, 256), S("wp", 256, 384)
    wrap(sw0, wa, 0)
    get(S("yw0", 0, K), I(S("raw", 0, K), S("rho")))
    get(S("b0"), I(S("thb"), S("n0", 0, KW)))
    get(S("a0"), I(S("b0"), S("rho")))
    get(S("yw0", K), I(S("raw", K), S("rho")), 0.125)
    get(S("b0s"), I(S("thb"), S("n0", KW)))
    send([([S("yw0")], STEP, S("yw1"))], own=opt["own"]["y"])
    send([([S("yw0")], 2 * STEP, S("yw2"))], own=opt["own"]["y"])
    gdma(S("tw", 0, W), S("thb"), False)
    fill(S("onf"), 1.0)
    keep(S("idf"), S("onf"), [[-1, 128]], AluOpType.is_equal, 0, 1)
    cp(S("idb"), S("idf"))
    ts(S("nib"), S("idf"), -1.0, mul)
    ts(S("nif"), S("idf"), -1.0, mul)
    for lo in (O1, O1 + K, O0 + K):
        iota(S("dw", lo, lo + K), [[1, 16], [16, KW]], lo, 0)
    iota(S("dw", O2, O2 + 512), [[1, 4], [16, 128]], 0, 0)
    act(S("dw", O2 + 512, O2 + 1024), S("dw", O2, O2 + 512), Ident, 1.0, 4.0)
    act(S("dw", O2 + 1024), S("dw", O2, O2 + 1024), Ident, 1.0, 8.0)
    ta = [S("n0", 0, KW), S("r1", 0, KW), S("r2", 0, KW)]
    tb = [S("nb0"), S("r1", KW), S("r2", KW)]

    def lookup(out, table, t, row, via=("lu1", "ls1", S("gw"))):
        for i, lst in enumerate((ta[t], tb[t])):
            cut = S(via[2][0], via[2][1] + i * KW, via[2][1] + (i + 1) * KW)
            get(S(via[i]), I(table, lst))
            wrap(cut, S(via[i]), row)
            tolist(S(out, i * KW, (i + 1) * KW), cut)

    lookup("f1", wa, 1, 0)
    put(wa, ta[1], S("dw", O1, O1 + K))
    put(wa, tb[1], S("dw", O1 + K, O2))
    wrap(sw1, wa, 0)
    lookup("f2", wa, 2, 0)
    tolist(S("dl"), sw1)
    put(wb, ta[2], S("dw", O0, O0 + K))
    put(wb, tb[2], S("dw", O0 + K, O1))
    wrap(l2, wb, 0)
    lookup("g1", wb, 1, 0, ("pa", "pb", S("wc", 256)))
    act(S("raw"), I(S("vab"), S("r2")))
    act(S("vaa"), I(S("raw", 0, K), S("rho")))
    act(S("vbs"), I(S("raw", K), S("rho")))
    ts(S("pf", 6, 7), S("pf", 0, 1), 128.0, mul)
    ts(S("rh2"), S("jw"), S("pf", 6, 7), plus)

    def overlay(out, below, sw, base, to):
        ts(S("fa"), sw, 0.5 - base, plus, 65536.0, mul)
        if to != base:
            ts(sw, sw, float(to - base), plus)
        tt(S("fa"), S("fa"), sw, AluOpType.min)
        tt(out, below, S("fa"), mx)

    overlay(l1, l2, sw1, O1, O1)
    overlay(lh, l1, sw0, O0, O2)
    for row, src in ((4, l1), (8, lh)):
        unwrap(wa, row, src, "unl")
    lookup("g0", wa, 0, 4)
    places(S("po2"), 128)
    act(wb, I(wa, S("po2")))
    wrap(sw0, wb, 8)
    tolist(S("hl"), sw0)
    send([([S("f1", KW)], -STEP, S("home", 0, KW)), ([S("g1", KW)], -STEP, S("home", KW, 2 * KW)),
          ([S("f2", KW)], -2 * STEP, S("home", 2 * KW))])
    rows = [4, 8, 12, 2, 6, 0]
    iota(S("j6"), [[0, 6], [int(JM), KW]], 0, 0)
    ts(S("pf", 2, 3), S("pf", 0, 1), KW * JM, mul)
    ts(S("j6"), S("j6"), S("pf", 2, 3), plus)
    cp(S("kw", 0, KW), S("rho"))
    cp(S("kw", KW, 2 * KW), S("g0", KW))
    cp(S("kw", 2 * KW, 5 * KW), S("home"))
    cp(S("kw", 5 * KW), S("cw", 0, KW))
    tt(S("kw"), S("kw"), S("j6"), plus)
    iota(S("kr"), [[0, K]], 0, 0)
    for i in range(6):
        unwrap(S("kr"), rows[i], S("kw", i * KW, (i + 1) * KW), "unk0")
    iota(S("one"), [[0, H]], 1, 0)
    fill(S("bm"), -33.0 * 2 ** 17)
    fill(S("vm"), 2.0 ** 25)
    keep(S("vm"), S("vm"), [[-16, 8], [0, 16]], AluOpType.is_ge, 0, 1)
    keep(S("vm"), S("vm"), [[16, 8], [0, 16]], AluOpType.is_gt, 32, -1)
    add("v", lambda g, T, c: g.vector.memset(T.vm[0:16, 112:128], 2.0 ** 25), [], [S("vm", 112)], lambda m: 0.13)
    keep(S("onf"), S("onf"), [[-16, 8], [0, 16]], AluOpType.is_ge, 0, 1)
    keep(S("onf"), S("onf"), [[16, 8], [0, 16]], AluOpType.is_gt, 16, -1)
    ts(S("hot"), S("jw", 0, 16), S("pf", 0, 1), AluOpType.is_equal)
    ts(S("jw"), S("idf"), -2.0, mul)

    def c_(name, c, base=0):
        return S(name, base + c[0], base + c[1])

    def o_(x, c):
        return S(x[0], x[1] + c[0] // 16, x[1] + c[1] // 16)

    main[0] = True
    two = [(0, H), (H, K)]
    three = [(0, opt["head"]), (opt["head"], H), (H, K)]

    def vv(name, out, x, y, op):
        def at(v, c):
            if isinstance(v, str):
                return c_(v, c, PO if v.startswith("ps") else 0)
            return I(v[0], o_(v[1], c)) if isinstance(v[0], tuple) else c_(v[0], c, v[1])
        for c in [(0, K)] if name in opt["wide"] else two:
            tt(at(out, c), at(x, c), at(y, c), op)

    def pe(P, *terms):
        for c in two:
            mms([(c_(P, c, PO), S(mat), S("one") if x == "one" else c_(x, c, lo), i == 0, i == len(terms) - 1)
                 for i, (mat, x, lo) in enumerate(terms)])

    def adds(name, out, src):
        out = (out, 0) if isinstance(out, str) else out
        for c in two if name in opt["half"] else [(0, K)]:
            gdma(c_(out[0], c, out[1]), c_(src, c))

    def square(out, x):
        act(S(out, PO, PO + K) if out.startswith("ps") else S(out, 0, K), S(x), Square)

    def picks(name, out, win, lst, cs):
        for c in [(0, K)] if name in opt["wide"] else cs:
            act(c_(out, c), I(win, o_(lst, c)))

    for k in range(RO):
        last = k == RO - 1
        R = ["ps%d" % ((i + k) % 4) for i in range(4)]
        if k == 0:
            fb = [None, S("f1", KW), S("f2", KW)]; gb = [S("g0", KW), S("g1", KW)]
        else:
            fb = [None, S("v1%d" % k, 0, KW), S("v2%d" % k, 0, KW)]; gb = [S("lw%d" % k, KW, 2 * KW), S("v1%d" % k, KW)]
        fa = [None, S("f1", 0, KW), S("f2", 0, KW)]; ga = [S("g0", 0, KW), S("g1", 0, KW)]
        bn = ["b0s" if k == 0 else "b0", "b1", "b2"]
        vb = "vbs" if k == 0 else "vbb"
        lu, ls = "lu%d" % (k % 2), "ls%d" % (k % 2)
        cof = [("aa0", "bb0"), ("aa1", "bb1"), ("u1", "db")]

        def back(win, base, t):
            if k > 0:
                act(S(win, base, base + K), I(S("bt"), S("x%d%d" % (t, k))))

        for t in range(TV):
            E, C, X = R[1 if t != 1 else 0], R[2], R[3]
            a, b, yw, ab, ea, eb = "a%d" % t, bn[t], "yw%d" % t, "ab%d" % t, "ea%d" % t, "eb%d" % t
            pe3 = last and t == 2
            pe(C, ("nib", yw, K))
            if t == 0:
                win, lst = (S("thb"), S("n0", KW)) if k == 0 else (S("b0s"), S("lw%d" % k, 5 * KW))
            else:
                win, lst = S("tw", 0, O1 if t == 1 else O2), fb[t]
                picks("", a, win, fa[t], three)
            if t > 0 or k > 0:
                picks("fb", b, win, lst, two)
            if t == 2:
                if k == 0:
                    act(S("thb"), I(S("vab"), S("rh2")))
                act(S("dw", 0, W), I(S("tw"), S("dl")), scale=-1.0)
                gdma(S("dw", 0, W), S("thb"))
                if k > 0:
                    act(S("vbb"), I(S("vbs"), S("v2%d" % k, KW)))
            base = O0 + 2 * K * t
            if t == 0 and str(k) in opt["pa0"]:
                pe(R[0], ("idb", a, 0))
                vv("", ab, b, R[0], mul)
            else:
                for c in (three if t > 0 else two):
                    tt(c_(ab, c), I(win, o_(lst, c)), c_(a, c), mul)
            pe(E, ("idf", ab, 0), ("nib", yw, 0))
            vv("ea", ea, E, a, mul)
            if pe3:
                for P, v, x in ((R[3], vb, b), (R[0], "vaa", a)):
                    for c in two:
                        mms([(c_(P, c, PO), S("idb"), c_(v, c), True, False), (c_(P, c, PO), S("nif"), c_(x, c), False, False)])
            if pe3 or (last and "b" in opt["fd"]):
                vv("tb", "bt", ea, C, mul)
                if not pe3:
                    adds("fb", "bt", b)
            else:
                vv("tb", X, ea, C, mul)
                vv("bn", ("tw", base + K) if k == 0 and t < 2 else "bt", b, X, plus)
            if t < 2:
                back("tw", base + K, t)
            vv("eb", eb, E, b, mul)
            if pe3:
                vv("ta", "q1", eb, C, mul)
                for P, x in ((R[3], "bt"), (R[0], "q1")):
                    for c in two:
                        mms([(c_(P, c, PO), S("nif"), c_(x, c), False, True)])
            elif last and "a" in opt["fd"]:
                vv("ta", ("tw", base), eb, C, mul)
                adds("fa", ("tw", base), a)
            else:
                Y = X if last else C
                vv("ta", Y, eb, C, mul)
                vv("an", ("tw", base) if t < 2 else "q1", a, Y, plus)
            if last:
                pe(E, ("jw", ab, 0), ("idb", yw, 0))
                vv("cm", ab, (yw, K), E, mul)
                for sq, x in zip(cof[t], (a, b)):
                    square(sq, x)
                    vv("cf", sq, sq, C, mul)
                    if t == 2:
                        act(S(sq, 0, K), S(sq, 0, K), Ident, 1.0, 1.0)
            elif t > 0:
                if str(t) in opt["m_dma"]:
                    for c in two:
                        act(c_("xs", c), c_(E, c, PO))
                    adds("m", ab, "xs")
                else:
                    vv("m", ab, ab, E, plus)
        for t in range(TV - 1, -1, -1):
            a, b, yw, ab, ea, eb = "a%d" % t, bn[t], "yw%d" % t, "ab%d" % t, "ea%d" % t, "eb%d" % t
            base = O0 + 2 * K * (2 - t)
            outb, outa = ("dw", base + K) if k == 0 else "bt", ("dw", base)
            win = S("dw", 0, O1 if t == 1 else O2)
            if t == 2 and not last:
                DA, DB, Wt, Q = R[2], R[3], R[0], R[1]
                pe(DB, ("nif", "bt", 0), ("idb", vb, 0))
                pe(DA, ("nif", "q1", 0), ("idb", "vaa", 0))
                square("aa0", a)
                square("bb0", b)
                if opt["mid2"]:
                    pe(Wt, ("idb", yw, K))

                def first(n, sq, D1, D2, t2, P):
                    vv("p" + n, sq, sq, D1, mul)
                    if n in opt["mid2"]:
                        vv("p" + n, t2, ab, D2, mul)
                        adds("s" + n, sq, t2)
                    else:
                        vv("p" + n, P, ab, D2, mul)

                def second(n, sq, D1, P, out):
                    if n in opt["mid2"]:
                        vv("w", sq, sq, Wt, mul)
                    else:
                        vv("w", P, sq, P, plus)
                        vv("w", sq, (yw, K), P, mul)
                    vv("w", out, D1, sq, minus)

                def terms():
                    vv("t2", "pa", eb, DA, mul)
                    vv("t2", "pb", ea, DB, mul)
                    send([([S("pa"), S("pb")], -2 * STEP, S(lu))], own=opt["own"]["t2"])
                Qa = Q if opt["mid2"] else Wt
                steps = dict(b=lambda: first("b", "aa0", DB, DA, "xs", Q), a=lambda: first("a", "bb0", DA, DB, "q1", Qa), t=terms,
                             B=lambda: (second("b", "aa0", DB, Q, outb), back("dw", base + K, t)),
                             A=lambda: second("a", "bb0", DA, Qa, outa))
                for x in opt["ord2"]:
                    steps[x]()
            elif t == 1 and not last:
                AA, M, BB, Wt = R[1], R[3], R[0], R[2]
                square(AA, a)
                pe(M, ("idf", ab, 0))
                square(BB, b)
                if opt["mid1"]:
                    pe(Wt, ("idb", yw, K))
                picks("db", "db", win, gb[t], two)
                picks("da", "da", win, ga[t], two)

                def first(n, P, d1, d2, t1, t2):
                    if n in opt["mid1"]:
                        vv("p" + n, t1, d1, P, mul)
                        vv("p" + n, t2, d2, M, mul)
                        adds("s" + n, t1, t2)
                    else:
                        vv("p" + n, P, d1, P, mul)
                        vv("p" + n, t2, d2, M, mul)

                def second(n, P, d1, t1, t2, out):
                    if n in opt["mid1"]:
                        vv("w", P, t1, Wt, mul)
                    else:
                        vv("w", P, t2, P, plus)
                        vv("w", P, (yw, K), P, mul)
                    vv("w", out, d1, P, minus)
                steps = dict(b=lambda: first("b", AA, "db", "da", "aa1", "xs"), a=lambda: first("a", BB, "da", "db", "bb1", "aa0"),
                             u=lambda: vv("u", "u1", (win, gb[t]), ea, mul), q=lambda: vv("u", "q1", (win, ga[t]), eb, mul),
                             t=lambda: send([([S("u1"), S("q1")], -STEP, S(ls))], own=opt["own"]["t1"]),
                             B=lambda: (second("b", AA, "db", "aa1", "xs", outb), back("dw", base + K, t)),
                             A=lambda: second("a", BB, "da", "bb1", "aa0", outa))
                for x in opt["ord1"]:
                    steps[x]()
            elif not last:
                P, L, Z = R[3], R[1], R[2]
                pe(P, ("idf", eb, 0))
                pe(L, ("nif", lu, 0))
                for c in two:
                    mms([(c_(Z, c, PO), S("bm"), S("one"), True, False)])
                picks("", "da", win, ga[t], two)
                vv("u", "xs", (win, gb[t]), ea, mul)
                vv("h", P, P, "da", mul)
                vv("h", "xs", P, "xs", plus)
                vv("h", L, L, ls, minus)
                vv("up", "up", "xs", L, AluOpType.is_gt)
            elif t == 2:
                DA, DB, Q = R[0], R[3], R[1]

                def side(n, sq, D1, D2, t2, out):
                    if n in opt["fin"][t]:
                        vv("p3", out, sq, D1, mul)
                        vv("p3", t2, ab, D2, mul)
                        adds("z" + n, out, t2)
                    else:
                        vv("p3", sq, sq, D1, mul)
                        vv("p3", Q, ab, D2, mul)
                        vv("p3", out, sq, Q, plus)

                def terms():
                    vv("t2", "pa", eb, DA, mul)
                    vv("t2", "pb", ea, DB, mul)
                    send([([S("pa"), S("pb")], -2 * STEP, S(lu))], own=opt["own"]["t2"])
                steps = dict(b=lambda: (side("b", cof[t][0], DB, DA, "xs", outb), back("dw", base + K, t)),
                             a=lambda: side("a", cof[t][1], DA, DB, "q1", outa), t=terms)
                for x in opt["ord3"][t]:
                    steps[x]()
            else:
                CB, CA, CM = (R[2], R[1], R[3]) if t == 1 else (R[0], R[2], R[3])
                pe(CB, ("idf", cof[t][0], 0), ("idb", "one", 0))
                pe(CA, ("idf", cof[t][1], 0), ("idb", "one", 0))
                pe(CM, ("idf", ab, 0))
                picks("db", "db", win, gb[t], two)
                picks("da", "da", win, ga[t], two)
                u, q = ("u1", "q1") if t == 1 else ("lu1", "ls1")

                def side(n, P, d1, d2, t2, out):
                    if n in opt["fin"][t]:
                        vv("p3", out, d1, P, mul)
                        vv("p3", t2, d2, CM, mul)
                        adds("z" + n, out, t2)
                    else:
                        vv("p3", P, d1, P, mul)
                        vv("p3", t2, d2, CM, mul)
                        vv("p3", out, t2, P, plus)

                def terms():
                    if t == 1:
                        send([([S(u), S(q)], -STEP, S(ls))], own=opt["own"]["t1"])
                        return
                    gdma(S(lu), S(u))
                    for c in two:
                        mms([(c_(R[1], c, PO), S("idb"), S("one"), True, False), (c_(R[1], c, PO), S("nib"), S("one"), False, False)])
                    for x in (q, lu, ls):
                        for c in range(2):
                            mms([(S(R[1], PO + s * KW, PO + (s + 1) * KW), S("idf"), (x, s, K, 16), False, x == ls and s % 8 == 7)
                                 for s in range(8 * c, 8 * c + 8)])
                    for c in two:
                        act(c_("pa", c), c_(R[1], c, PO), scale=0.125)
                    dma(lambda T: T.yh[:], lambda T: T.pa[:], [S("pa")], [], 500e3)
                steps = dict(b=lambda: (side("b", CB, "db", "da", "xs", outb), back("dw", base + K, t)),
                             a=lambda: side("a", CA, "da", "db", "a2", outa), t=terms,
                             u=lambda: vv("u", u, (win, gb[t]), ea, mul), q=lambda: vv("u", q, (win, ga[t]), eb, mul))
                for x in opt["ord3"][t]:
                    steps[x]()
        if last:
            n = opt["outs"]
            for c in range(len(n)):
                lo, hi = c * W // len(n), (c + 1) * W // len(n)
                out, src = S("wf", lo, hi), I(S("dw", 0, O2 + 2 * K), S("hl", lo // 16, hi // 16))
                if n[c] == "v":
                    ts(out, src, -1.0, mul)
                else:
                    act(out, src, scale=-1.0)
                dma(lambda T, lo=lo, hi=hi: T.yd[:, lo:hi], lambda T, lo=lo, hi=hi: T.wf[:, lo:hi], [out], [], 1050e3 / len(n),
                    q="y" if n[c] == "v" else "s")
            break
        n = k + 1; lw = "lw%d" % n
        fill(S("da", 0, 1), LOW)
        mms([(S(Z, PO + s * KW, PO + (s + 1) * KW), S("vm"), ("up", s, K, 16), False, s % 8 == 7) for s in range(16)])
        scan(S("da", 1, K + 1), S(Z, PO, PO + K), S("kr"), LOW)
        ts(S("end"), S("hot"), S("da", K, K + 1), mul, LOW / 16, plus)
        mms([(S(Z, 0, 16), S("onf"), S("end"), True, True)])
        for lists, grp in (([5], "p%d" % n), ([0], "i%d" % n), ([1, 2, 3, 4], "o%d" % n)):
            for i in lists:
                wrap(S("wp", i * KW, (i + 1) * KW), S("da", 0, K), rows[i], grp)
                wrap(S("wc", i * KW, (i + 1) * KW), S("da", 1, K + 1), rows[i], grp, "s" if i == 5 else "y")
            lo, hi = lists[0] * KW, (lists[-1] + 1) * KW
            tt(S("wp", lo, hi), S("wp", lo, hi), S("wc", lo, hi), minus)
            tt(S("wp", lo, hi), S("wp", lo, hi), S("kw", lo, hi), plus)
            for i in lists:
                ts(S("br", i * KW, (i + 1) * KW), S("wp", i * KW, (i + 1) * KW), S(Z, rows[i], rows[i] + 1), mx)
            ts(S("br", 400 + lo, 400 + hi), S("br", lo, hi), int(JM) - 1, AluOpType.bitwise_and)
            cp(S(lw, lo, hi), S("br", 400 + lo, 400 + hi))
        send([([S(lw, 2 * KW, 4 * KW)], STEP, S("v1%d" % n)), ([S(lw, 4 * KW)], 2 * STEP, S("v2%d" % n))], also=[S(lu), S(ls)])
        act(I(S("q1"), S(lw, 0, KW)), S("vj"), Silu)
        wrap(S("iw"), S("q1"), 0)
        tolist(S("x0%d" % n), S("iw"), O0 + K)
        send([([S("x0%d" % n)], STEP, S("x1%d" % n)), ([S("x0%d" % n)], 2 * STEP, S("x2%d" % n))])
        if n < RO - 1:
            tt(S("kw"), S("br", 400, 400 + 6 * KW), S("j6"), plus)
            for i in range(6):
                unwrap(S("kr"), rows[i], S("kw", i * KW, (i + 1) * KW), "unk%d" % n)
    mem = {}
    for i, o in enumerate(ops):
        if o["group"] is not None:
            mem.setdefault(o["group"], []).append(i)
    for o in ops:
        full = set()
        for j in o["deps"]:
            full.update(mem[ops[j]["group"]] if ops[j]["group"] is not None else [j])
        o["deps"] = sorted(full)
    return ops, sems, mem, relays


def times(ops, m):
    cost = [o["cost"](m) for o in ops]
    ways = [o["lat"](m) if o["lat"] else [] for o in ops]
    lat = [max([a + b + max(c, 0.0) for a, r, b, c in w] + [0.0]) for w in ways]
    gap = [0.0 if o["kind"] == "r" else m["hop"] for o in ops]
    return cost, lat, gap, ways


def replay(ops, seq, tm):
    cost, lat, gap, ways = tm
    free, st, fin, arr = {}, [0.0] * len(ops), [0.0] * len(ops), {}
    for i in seq:
        o = ops[i]; s = free.get(o["q"], 0.0)
        for d in o["deps"]:
            if fin[d] + gap[i] > s:
                s = fin[d] + gap[i]
        if o["q"] != "-":
            free[o["q"]] = s + cost[i]
        elif arr.get(o["deps"][0], 0.0) > s:
            s = arr[o["deps"][0]]
        st[i] = s; s += cost[i]; f = s
        for a, r, b, c in ways[i]:
            e = max(s + a, free.get(r, 0.0)) + b
            if r:
                free[r] = e
            if c < 0:
                arr[i] = e
            elif e + c > f:
                f = e + c
        fin[i] = f
    return st, fin


def place(qs, links, turn, pre, cost, post):
    n = len(qs); busy, st, fin = {}, [0.0] * n, [0.0] * n
    for i in turn:
        s = 0.0
        for d in links[i]:
            if fin[d] > s:
                s = fin[d]
        s += pre[i]; c = cost[i]
        if qs[i] != "-":
            line = busy.setdefault(qs[i], []); p = len(line)
            while p > 0 and line[p - 1][1] > s:
                p -= 1
            while p < len(line) and line[p][0] < s + c:
                if line[p][1] > s:
                    s = line[p][1]
                p += 1
            line.insert(p, (s, s + c))
        st[i] = s; fin[i] = s + c + post[i]
    return st


def order(ops, tries, seed=1):
    tms = [times(ops, m) for m in SPREAD]; rng = np.random.default_rng(seed); n = len(ops)
    qs = [o["q"] for o in ops]; before = [o["deps"] for o in ops]; after = [[] for o in ops]
    for i, o in enumerate(ops):
        for d in o["deps"]:
            after[d].append(i)

    def forth(key, tm):
        key = list(key)
        for i in range(n - 1, -1, -1):
            for d in before[i]:
                if key[i] < key[d]:
                    key[d] = key[i]
        st = place(qs, before, sorted(range(n), key=lambda i: (key[i], i)), tm[2], tm[0], tm[1])
        return sorted(range(n), key=lambda i: (st[i], i))

    def late(seq, tm):
        st, fin = replay(ops, seq, tm)
        st = place(qs, after, sorted(range(n), key=lambda i: (-fin[i], -i)), [fin[i] - st[i] - tm[0][i] for i in range(n)], tm[0], tm[2])
        return [-(st[i] + tm[0][i]) for i in range(n)]

    def value(seq, bar=1e9):
        total = 0.0
        for j, tm in enumerate(tms):
            total += max(replay(ops, seq, tm)[1])
            if j == 0 and total > bar:
                return 1e9, 1e9
            first = total if j == 0 else first
        return total, first

    best = None
    for pace in (1.0, 1.2, 1.45, 2.0):
        cost, lat, gap, ways = tms[0]; now = 0.0; key = [1e9] * n
        for i, o in enumerate(ops):
            if o["main"]:
                key[i] = now; now += pace * cost[i]
        for i in range(n - 1, -1, -1):
            key[i] = min(key[i], now)
            for d in before[i]:
                key[d] = min(key[d], key[i] - pace * cost[d] - lat[d] - gap[i])
        for rep in range(6):
            seq = forth(key, tms[0]); val = value(seq)
            if best is None or val[0] < best[0][0]:
                best = (val, seq, key)
            key = late(seq, tms[0])
    for it in range(tries):
        if it % 100 == 0:
            key = late(best[1], tms[0])
        else:
            key = list(best[2])
            for j in rng.integers(0, n, 1 + it % 3):
                key[j] += float(rng.normal()) * (0.5, 2.0, 8.0)[it % 3]
        seq = forth(key, tms[0]); val = value(seq, best[0][1] + 1.5)
        if val[0] <= best[0][0]:
            best = (val, seq, key)
    return best[1]


OPS, SEMAPHORES, MEM, RELAYS = build(OPT)
SEQ = order(OPS, TRIES)


def rank_program(g, core, T, topo):
    rank = T.rank_of(core)
    if rank is None:
        served = [r for r, c in enumerate(T.cores) if topo.chip(c) == topo.chip(core) and helper(T, topo, c) == core]
        sent = 0
        for i, step, hold, land in sorted(RELAYS, key=lambda x: SEQ.index(x[0])) if served else []:
            dst = T.cores[(served[0] + step) % N]; rid, pid, _ = topo.addr(dst)
            g.wait_ge(T.sem["h%d" % i], 8)
            g.remote_dma(ap(T, land), ap(T, hold), T.sem["a%d_%d" % (i, step % N)], T.sem.hand, pid, rid,
                         sum(1 << e for e in topo.engines(core, dst)[:8]))
            sent += 8
        if sent:
            g.wait_ge(T.sem.hand, sent)
        return
    ctx = dict(rank=rank, core=core, topo=topo)
    queue = {"v": g.vector, "s": g.scalar, "t": g.tensor, "g": g, "y": g.sync}
    count, mark, seen, top = {}, {}, {}, {}
    for i in SEQ:
        o = OPS[i]
        if o["kind"] == "c":
            sem = "c" + o["q"]; count[sem] = count.get(sem, 0) + 1
            mark[i] = (sem, count[sem])
        else:
            mark[i] = (o["group"], sum(OPS[j]["cnt"] for j in MEM[o["group"]]))
            count[o["group"]] = mark[i][1]
        if o["kind"] == "r":
            continue
        need = {}
        for j in o["deps"]:
            sem, v = mark[j]
            need[sem] = max(need.get(sem, 0), v)
        for sem, v in sorted(need.items()):
            if seen.get((o["q"], sem), 0) < v:
                queue[o["q"]].wait_ge(T.sem[sem], v)
                seen[(o["q"], sem)] = v; top[sem] = max(top.get(sem, 0), v)
        ins = o["fn"](g, T, ctx)
        if o["kind"] == "c":
            ins.then_inc(T.sem[mark[i][0]], 1)
        elif o["kind"] == "d":
            ins.then_inc(T.sem[o["group"]], 16)
    for sem, v in sorted(count.items()):
        if top.get(sem, 0) < v:
            g.wait_ge(T.sem[sem], v)
